import numpy as np, ml_dtypes
CORES = [2,6,10,14,18,22,26,30]
N = 8
import mx_ref
BF = ml_dtypes.bfloat16
def entries(a):
    return np.ascontiguousarray(a.T).reshape(-1)
def table(e):
    return np.ascontiguousarray(np.reshape(e, (-1, 16)).T).astype(np.int32)
def f(rng, *shape):
    return mx_ref.flush((rng.standard_normal(shape, dtype=np.float32) * np.exp2(rng.integers(-2, 3, shape[:-1] + (1,)))).astype(BF))
def wide(rng, *shape, cols=0):
    v = rng.standard_normal(shape, dtype=np.float32) * np.exp2(rng.integers(-12, 13, shape)).astype(np.float32)
    if cols: v *= np.repeat(np.exp2(rng.integers(-cols, cols + 1, shape[:-2] + (1, shape[-1] // 4))) * (rng.random(shape[:-2] + (1, shape[-1] // 4)) > 0.0625), 4, axis=-1).astype(np.float32)
    return mx_ref.flush(v.astype(BF))
T, ND, CD, LM, CAPP = 1024, 64, 16, 64, 160
def lens(rng, n, total):
    a = 1 + np.minimum(LM - 1, rng.multinomial(total - n, rng.dirichlet(np.ones(n))))
    for i in rng.permutation(n): a[i] += min(LM - a[i], total - a.sum())
    return a
def places(rng, l):
    o = rng.permutation(ND); g = rng.multinomial(T - l.sum(), rng.dirichlet(np.ones(ND + 1)))
    s = np.zeros(ND, int); s[o] = np.cumsum(g[:ND]) + np.cumsum(l[o]) - l[o]
    return s
def pick(rng, l):
    p = rng.permutation(ND); a, b = p[:CD].copy(), p[CD:].copy()
    while l[a].sum() > CAPP:
        i = np.argmax(l[a]); j = rng.choice(np.flatnonzero(l[b] < l[a[i]]))
        a[i], b[j] = b[j], a[i]
    return rng.permutation(a)
def lists(rng, kind="any"):
    s, n, c = [], [], np.zeros((N, N * CD), int)
    K, J = (T - ND) // (LM - 1), (CAPP - CD) // (LM - 1)
    TT = min(T, ND // CD * CAPP)
    for q in range(N):
        d = rng.permutation(ND); l = np.ones(ND, int)
        if kind == "long": l[d[:K]] = LM
        elif kind == "full": l[d] = np.concatenate([lens(rng, CD, CAPP), lens(rng, CD, CAPP), lens(rng, ND - 2 * CD, T - 2 * CAPP)])
        elif kind == "any": l[d] = lens(rng, ND, int(rng.integers(TT - TT // 4, TT + 1)))
        s.append(table(places(rng, l))); n.append(table(l))
        for r in range(N):
            if kind == "long": e = rng.permutation(np.concatenate([rng.permutation(d[:K])[:J], rng.permutation(d[K:])[:CD - J]]))
            elif kind == "full": k = CD * int(rng.integers(0, 2)); e = rng.permutation(d[k:k + CD])
            else: e = pick(rng, l)
            c[r, CD * q:CD * q + CD] = e
    return {"st": np.stack(s), "ln": np.stack(n), "cd": np.stack([table(c[r]) for r in range(N)])}
def setup_inputs(rng):
    return {"x": f(rng, N, 128, 4 * T), "qw": f(rng, N, 128, 512), **lists(rng)}
def setup_inputs_long(rng):
    return {**setup_inputs(rng), **lists(rng, "long")}
def setup_inputs_ones(rng):
    return {**setup_inputs(rng), **lists(rng, "ones")}
def setup_inputs_full(rng):
    return {**setup_inputs(rng), **lists(rng, "full")}
def setup_inputs_below(rng):
    d = setup_inputs(rng); p = rng.permutation(N)
    s, u = rng.integers(-20, 27, N), rng.integers(-20, 28, N)
    s[p[0]] = 26; u[rng.choice(p[:-1])] = 27; s[p[-1]] = 0; u[p[-1]] = 0
    d["x"] = mx_ref.flush((-np.exp2(rng.uniform(-3, 3, (N, 128, 4 * T)) + s[:, None, None])).astype(BF))
    d["qw"] = mx_ref.flush(np.exp2(rng.uniform(-2, 2, (N, 128, 512)) + u[:, None, None]).astype(BF))
    return d
def setup_inputs_spread(rng):
    d = setup_inputs(rng); d["x"] = wide(rng, N, 128, 4 * T, cols=8); return d
def check_inputs(d):
    b = []
    L = [entries(d["ln"][r]).astype(np.int64) for r in range(N)]
    for r in range(N):
        s, l = entries(d["st"][r]).astype(np.int64), L[r]
        if l.min() < 1 or l.max() > LM: b.append("ln")
        o = np.argsort(s, kind="stable")
        if s.min() < 0 or (s + l).max() > T or (s[o][:-1] + l[o][:-1] > s[o][1:]).any(): b.append("st")
        c = entries(d["cd"][r])
        if c.min() < 0 or c.max() >= ND: b.append("cd"); continue
        for q in range(N):
            e = c[CD * q:CD * q + CD]
            if len(set(e.tolist())) != CD or L[q][e].sum() > CAPP: b.append("cd")
    return sorted(set(b))
def reference(x, qw, st, ln, cd):
    X = [mx_ref.quantize(x[q]) for q in range(N)]
    y = np.zeros((N, 128, N * CD), np.float32)
    for r in range(N):
        W = mx_ref.quantize(qw[r]); c = entries(cd[r])
        for q in range(N):
            z = mx_ref.matmul(W, X[q]); s, l = entries(st[q]), entries(ln[q])
            for i in range(CD * q, CD * q + CD):
                y[r][:, i] = z[:, s[c[i]]:s[c[i]] + l[c[i]]].max(axis=1)
    return {"y": y}

@@ -1,0 +1,314 @@
+from concourse.bass import DstId, RemoteDMATransfer
+from concourse.mybir import dt, AluOpType, ActivationFunctionType
+
+N, CD, CAP, XC = 8, 16, 160, 1024
+XW = XC + CAP
+NEG = -5.0e29
+W = N * CD
+
+SCRATCH = {k: ("sbuf", [128, w], t) for t, ks in {
+    "int32": {"cd8": 8, "cdl": 32, "sl": 128, "ip": 1, "ci": 1, "ei": W, "ph": W},
+    "float32": {"row": 192, "tab": 192, "cf": 8, "kk": 24, "rst": W, "sb": W, "zz": W, "cc": W,
+                "lnf": W, "eb": W + 4, "cmpb": W + 4, "bs": W + 4, "ix": W, "jp": W, "mk": W, "gm": W, "gg": W, "hh": W,
+                "t1": W + 4, "t2": W, "raw": 16, "tin": 32, "tout": 32, "ef": 16,
+                "msk": 8 * CAP + 8, "neg": 128, "z": 8 * CAP, "ys": 128},
+    "uint16": {"cu": 8, "iu": 8, "of0": W, "of1": W, "of2": W, "of3": W, "eu": 16},
+    "bfloat16": {"xs": 4 * XW, "h": 32 * CAP, "qs": 512},
+    "float8_e4m3fn_x4": {"qc": 8 * CAP, "wc": 128, "rc": 8 * CAP},
+    "uint8": {"qp": 8 * CAP, "wp": 128, "rp": 8 * CAP}}.items() for k, w in ks.items()}
+SCRATCH["es"] = ("dram", [128, 1], "float32")
+SCRATCH["el"] = ("dram", [8, 128, 1], "float32")
+SCRATCH["ps"] = ("psum", [128, 4 * 512], "float32")
+SEMAPHORES = (["ldc", "ldt", "ldx", "ldq", "gi", "pb", "vt", "xgo", "vz", "ca", "cb", "est", "er", "ell", "wq", "yd", "ls", "vv", "rw",
+               "e0", "e1", "e2"]
+              + [n + str(s) for n in ("hg", "qz", "ar") for s in range(8)]
+              + [n + str(s) for n in ("pm", "yg") for s in range(4)]
+              + ["of%d%d" % (b, t) for b in (0, 1) for t in range(4)] + ["m%d_%d" % (b, k) for b in (0, 1) for k in range(3, 16)])
+
+SCALAR = [(0, 1), (0, 1, 2, 3), (0, 1, 2), (0, 1), (0, 1, 2), (0, 1), (0, 1, 2, 3), (0, 1)]
+
+
+def rank_program(g, core, T, topo):
+    me = T.rank_of(core)
+    if me is None:
+        return
+    A, F = AluOpType, ActivationFunctionType
+    v, sc, sy, pe = g.vector, g.scalar, g.sync, g.tensor
+    S = T.sem
+    cores = list(T.cores)
+
+    def dist(a, b):
+        ca, cb = topo.chip(a), topo.chip(b)
+        if ca == cb:
+            return 3
+        if topo.mates(ca, cb):
+            return 2
+        return 1 if topo.same_plane(ca, cb) else 0
+
+    def chipmates(c):
+        return [r for r in range(N) if topo.chip(cores[r]) == topo.chip(c)]
+
+    def slot(a, b):
+        return 2 * dist(cores[a], cores[b]) + chipmates(cores[b]).index(b)
+
+    rank_at = [None] * N
+    for r in range(N):
+        rank_at[slot(me, r)] = r
+    own = slot(me, me)
+    par = [s for s in (6, 7) if s != own][0]
+    far_e = topo.engines(core, cores[rank_at[0]])
+    near_e = [e for e in topo.engines(core, cores[rank_at[par]]) if e not in far_e]
+
+    def msk(es):
+        m = 0
+        for e in es:
+            m |= 1 << e
+        return int(m)
+
+    sent = [0]
+
+    def tr(s, es, sem, src, dst):
+        rid, pid, _ = topo.addr(cores[rank_at[s]])
+        sent[0] += len(es)
+        return RemoteDMATransfer(dst_ids=[DstId(rid=rid, pnc=pid)], dma_engine_mask=msk(es), remote_sem=S[sem], src=src, dst=dst)
+
+    def there(s):
+        return slot(rank_at[s], me)
+
+    for k in range(8):
+        (sy if k % 2 == 0 else sc).dma_start(T.cd8[16 * k:16 * k + 16, :], T.cd[:, :]).then_inc(S.ldc, 16)
+    sy.dma_start(T.sl[0:1, 0:64], T.st[:, :]).then_inc(S.ldt, 16)
+    sc.dma_start(T.sl[0:1, 64:128], T.ln[:, :]).then_inc(S.ldt, 16)
+    sy.dma_start(T.xs[:, 0:1024], T.x[:, 0:1024]).then_inc(S.ldx, 16)
+    sc.dma_start(T.xs[:, 1024:2048], T.x[:, 1024:2048]).then_inc(S.ldx, 16)
+    sy.wait_ge(S.xgo, 1)
+    sy.dma_start(T.xs[:, 2048:3072], T.x[:, 2048:3072]).then_inc(S.ldx, 16)
+    sc.wait_ge(S.xgo, 1)
+    sc.dma_start(T.xs[:, 3072:4096], T.x[:, 3072:4096]).then_inc(S.ldx, 16)
+    sc.dma_start(T.qs[:, :], T.qw[:, :]).then_inc(S.ldq, 16)
+
+    g.iota(T.ip[:, 0:1], [[0, 1]], 0, 1).then_inc(S.gi, 1)
+    for out, pat, base in ((T.kk[:, 0:8], [[CAP, 8]], 0), (T.kk[:, 8:16], [[0, 4], [CAP, 2]], -1), (T.kk[:, 16:24], [[0, 2], [CD, 4]], 0),
+                           (T.cc[:, :], [[0, 8], [16, 16]], -16)):
+        g.iota(out, pat, base, 0, allow_small_or_imprecise_dtypes=True).then_inc(S.gi, 1)
+    g.wait_ge(S.ldc, 128)
+
+    def cdt(s, es, sem):
+        r, d = rank_at[s], there(s)
+        return tr(s, es, sem, T.cd8[:, r:r + 1], T.cdl[:, 4 * d:4 * d + 1])
+    g.remote_dma_fused([cdt(s, far_e[2 * s:2 * s + 2], "ca") for s in range(4)], local_sem=S.ls)
+    g.remote_dma_fused([cdt(4, far_e[0:4], "cb"), cdt(5, far_e[4:8], "cb"), cdt(par, near_e[0:4], "cb")], local_sem=S.ls)
+    g.sem_inc(S.xgo, 1)
+    g.wait_ge(S.vt, 1)
+    g.partition_broadcast(T.tab[:, 0:192], T.row[0:1, 0:192], 128).then_inc(S.pb, 1)
+
+    n = {"vv": 0}
+
+    def op(ins):
+        ins.then_inc(S.vv, 1)
+        n["vv"] += 1
+
+    def sync_v():
+        v.wait_ge(S.vv, n["vv"])
+
+    v.memset(T.xs[:, 4 * XC:4 * XW], 0.0).then_inc(S.vz, 1)
+    v.memset(T.raw[:, :], 0.0).then_inc(S.rw, 1)
+    op(v.memset(T.zz[:, :], 0.0))
+    op(v.memset(T.sb[:, :], 0.0))
+    op(v.memset(T.rst[:, :], 1.0))
+    for b in ("eb", "cmpb", "bs", "t1"):
+        op(v.memset(T[b][:, 0:1], 0.0))
+    v.wait_ge(S.gi, 5)
+    op(v.tensor_scalar(T.ci[:, 0:1], T.ip[:, 0:1], 15, None, A.bitwise_and))
+    sync_v()
+    op(v.tensor_copy(T.cf[:, 0:1], T.ci[:, 0:1]))
+    op(v.tensor_copy(T.rst[:, 0:W:CD], T.zz[:, 0:8]))
+    op(v.tensor_copy(T.sb[:, 0:W:CD], T.kk[:, 16:24]))
+    sync_v()
+    op(v.tensor_scalar(T.cf[:, 1:2], T.cf[:, 0:1], 16.0, -16.0, A.mult, A.add))
+    for t in range(4):
+        op(v.tensor_scalar(T.cf[:, 2 + t:3 + t], T.cf[:, 0:1], 4.0, float(t), A.mult, A.add))
+    v.wait_ge(S.ldt, 32)
+    for k in range(4):
+        op(v.tensor_copy(T.row[0:1, 16 * k:16 * k + 16], T.sl[0:1, k:64:4]))
+        op(v.tensor_copy(T.row[0:1, 64 + 16 * k:80 + 16 * k], T.sl[0:1, 64 + k:128:4]))
+    sync_v()
+    v.tensor_tensor(T.row[0:1, 128:192], T.row[0:1, 0:64], T.row[0:1, 64:128], A.add).then_inc(S.vt, 1)
+    v.wait_ge(S.ldc, 128)
+    op(v.tensor_copy(T.cdl[:, 4 * own:4 * own + 1], T.cd8[:, me:me + 1]))
+    op(v.memset(T.neg[:, :], NEG))
+    op(v.memset(T.msk[:, :], 0.0))
+    sync_v()
+    op(v.tensor_copy(T.msk[:, 0:8 * CAP:CAP], T.neg[:, 0:8]))
+    sync_v()
+
+    v.wait_ge(S.ca, 8)
+    v.wait_ge(S.cb, 12)
+    v.tensor_copy(T.cu[:, 0:8], T.cdl[:, 0:32:4]).then_inc(S.e0, 1)
+    v.wait_ge(S.pb, 1)
+    v.wait_ge(S.e0, 1)
+    v.tensor_copy(T.lnf[:, :], T.tab[:, 64:128].indirect(T.cu[:, 0:8])).then_inc(S.e1, 1)
+    v.wait_ge(S.e1, 1)
+    v.tensor_tensor_scan(T.eb[:, 1:W + 1], T.rst[:, :], T.lnf[:, :], 0.0, A.mult, A.add).then_inc(S.e2, 1)
+    v.wait_ge(S.e2, 1)
+
+    def lists(b, between=None):
+        lo, hi, c0, c1 = 64 * b, 64 * b + 64, 4 * b, 4 * b + 4
+
+        def m(k, ins):
+            ins.then_inc(S["m%d_%d" % (b, k)], 1)
+
+        def wm(*ks):
+            for k in ks:
+                v.wait_ge(S["m%d_%d" % (b, k)], 1)
+
+        m(3, v.tensor_copy(T.ei[:, lo:hi], T.eb[:, lo:hi]))
+        m(4, v.tensor_scalar(T.cmpb[:, lo + 1:hi + 1], T.eb[:, lo + 1:hi + 1], T.cf[:, 1:2], None, A.is_lt))
+        m(5, v.tensor_tensor(T.bs[:, lo + 1:hi + 1], T.tab[:, 128:192].indirect(T.cu[:, c0:c1]), T.eb[:, lo + 1:hi + 1], A.subtract))
+        wm(3)
+        m(6, v.tensor_scalar(T.ph[:, lo:hi], T.ei[:, lo:hi], 15, None, A.bitwise_and))
+        wm(4)
+        m(7, v.tensor_tensor_scan(T.ix[:, lo:hi], T.cmpb[:, lo:hi], T.sb[:, lo:hi], -1.0, A.add, A.max))
+        wm(5)
+        m(8, v.tensor_tensor(T.jp[:, lo:hi], T.bs[:, lo + 1:hi + 1], T.bs[:, lo:hi], A.subtract))
+        wm(6)
+        m(9, v.tensor_scalar(T.mk[:, lo:hi], T.ph[:, lo:hi], T.cf[:, 0:1], None, A.is_le))
+        wm(7)
+        m(10, v.tensor_copy(T.iu[:, c0:c1], T.ix[:, lo + CD - 1:hi:CD]))
+        wm(8, 9)
+        m(11, v.tensor_tensor(T.gm[:, lo:hi], T.jp[:, lo:hi], T.mk[:, lo:hi], A.mult))
+        wm(11)
+        m(12, v.tensor_tensor_scan(T.gg[:, lo:hi], T.zz[:, lo:hi], T.gm[:, lo:hi], 0.0, A.add, A.add))
+        wm(12)
+        m(13, v.tensor_tensor(T.hh[:, lo:hi], T.bs[:, lo + 1:hi + 1], T.gg[:, lo:hi], A.subtract))
+        if between is not None:
+            between()
+        wm(10, 13)
+        m(14, v.tensor_tensor(T.t1[:, lo + 1:hi + 1], T.hh[:, lo:hi].indirect(T.iu[:, c0:c1]), T.cc[:, lo:hi], A.add))
+        wm(14)
+        m(15, v.tensor_tensor(T.t2[:, lo:hi], T.gg[:, lo:hi].indirect(T.iu[:, c0:c1]), T.t1[:, lo:hi], A.add))
+        wm(15)
+        for t in range(4):
+            v.tensor_scalar(T["of%d" % t][:, lo:hi], T.t2[:, lo:hi], 4.0, T.cf[:, 2 + t:3 + t], A.mult, A.add).then_inc(S["of%d%d" % (b, t)], 1)
+
+    seen = {"s": [], "v": []}
+
+    def gather(key, s):
+        q = sc if key == "s" else v
+        role = 6 if s == own else 7 if s == par else s
+        for t in range(4):
+            if (t in SCALAR[role]) != (key == "s"):
+                continue
+            if not seen[key]:
+                q.wait_ge(S.ldx, 64)
+                q.wait_ge(S.vz, 1)
+            sem = "of%d%d" % (s // 4, t)
+            if sem not in seen[key]:
+                q.wait_ge(S[sem], 1)
+                seen[key].append(sem)
+            out, win = T.h[:, 640 * s + t:640 * s + 640:4], T.xs[:, 0:4 * XW].indirect(T["of%d" % t][:, CD * s + 2:CD * s + 12])
+            ins = sc.activation(out, win, F.Copy) if key == "s" else v.tensor_copy(out, win)
+            ins.then_inc(S["hg%d" % s], 1)
+
+    def quant(s):
+        v.wait_ge(S["hg%d" % s], 4)
+        cc, pp = (T.rc, T.rp) if s == own else (T.qc, T.qp)
+        v.quantize_mx(cc[:, CAP * s:CAP * s + CAP], pp[:, CAP * s:CAP * s + CAP], T.h[:, 640 * s:640 * s + 640]).then_inc(S["qz%d" % s], 1)
+
+    for s in (0, 1, 2, 3, 4, 5, par, own):
+        gather("s", s)
+
+    lists(0)
+    gather("v", 0)
+    quant(0)
+    gather("v", 1)
+    lists(1, lambda: quant(1))
+    for s in (2, 4):
+        gather("v", s)
+        gather("v", s + 1)
+        quant(s)
+        quant(s + 1)
+    gather("v", par)
+    v.wait_ge(S.ldq, 16)
+    v.quantize_mx(T.wc[:, :], T.wp[:, :], T.qs[:, :]).then_inc(S.wq, 1)
+    quant(par)
+    gather("v", own)
+
+    sy.wait_ge(S.e2, 1)
+    for d in range(4):
+        e0 = CD * rank_at[2 * d]
+        sy.dma_start(T.es[e0:e0 + 32, :], T.eb[0:1, 32 * d + 1:32 * d + 33]).then_inc(S.est, 16)
+    sy.dma_start(T.el[me, CD * me:CD * me + CD, :], T.eb[0:1, CD * own + 1:CD * own + CD + 1]).then_inc(S.est, 16)
+
+    g.wait_ge(S.est, 80)
+    ids = []
+    for s in [0, 1, 2, 3, 4, 5, par]:
+        rid, pid, _ = topo.addr(cores[rank_at[s]])
+        ids.append(DstId(rid=rid, pnc=pid))
+    g.remote_dma_fused([RemoteDMATransfer(dst_ids=ids, dma_engine_mask=msk(far_e[0:1]), remote_sem=S.er, srcs=[T.es[:, :]],
+                                          dsts=[T.el[me] for _ in ids])], local_sem=S.ls)
+    sent[0] += 1
+
+    def codes(s, es):
+        d = there(s)
+        return tr(s, es, "ar%d" % d, T.qc[:, CAP * s:CAP * s + CAP].bitcast(dt.uint8), T.rc[:, CAP * d:CAP * d + CAP].bitcast(dt.uint8))
+
+    def plane(s, es):
+        d = there(s)
+        return tr(s, es, "ar%d" % d, T.qp[:, CAP * s:CAP * s + CAP], T.rp[:, CAP * d:CAP * d + CAP])
+
+    for s in (0, 2, 4):
+        g.wait_ge(S["qz%d" % s], 1)
+        if s == 0:
+            g.remote_dma_fused([codes(0, far_e)], local_sem=S.ls)
+            g.wait_ge(S.qz1, 1)
+            g.remote_dma_fused([codes(1, far_e)], local_sem=S.ls)
+        else:
+            g.wait_ge(S["qz%d" % (s + 1)], 1)
+            g.remote_dma_fused([codes(s, far_e[0:4]), codes(s + 1, far_e[4:8])], local_sem=S.ls)
+        g.remote_dma_fused([plane(s, far_e[0:4]), plane(s + 1, far_e[4:8])], local_sem=S.ls)
+    g.wait_ge(S["qz%d" % par], 1)
+    g.remote_dma_fused([codes(par, near_e)], local_sem=S.ls)
+    g.remote_dma_fused([plane(par, near_e)], local_sem=S.ls)
+
+    sy.wait_ge(S.est, 80)
+    sy.wait_ge(S.er, 7)
+    sy.wait_ge(S.rw, 1)
+    for a in range(4):
+        sy.dma_start(T.raw[32 * a:32 * a + 8, :], T.el[:, CD * me:CD * me + CD, :]).then_inc(S.ell, 16)
+    v.wait_ge(S.ell, 64)
+    op(v.tensor_copy(T.tin[:, 0:16], T.raw[:, :]))
+    op(v.tensor_copy(T.tin[:, 16:32], T.raw[:, :]))
+    sync_v()
+    op(v.transpose(T.tout[:, :], T.tin[:, :]))
+    sync_v()
+    op(v.tensor_tensor(T.ef[:, 0:8], T.tout[:, 0:8], T.kk[:, 0:8], A.add))
+    op(v.tensor_tensor(T.ef[:, 8:16], T.tout[:, 0:8], T.kk[:, 8:16], A.add))
+    sync_v()
+    op(v.tensor_copy(T.eu[:, :], T.ef[:, :]))
+    sync_v()
+    op(v.tensor_copy(T.msk[:, :].indirect(T.eu[:, 0:8]), T.neg[:, :]))
+    quant(own)
+    sync_v()
+
+    pe.wait_ge(S.wq, 1)
+    order = [0, 1, 3, 2]
+    for c in order:
+        for s in (2 * c, 2 * c + 1):
+            if s == own:
+                pe.wait_ge(S["qz%d" % own], 1)
+            else:
+                pe.wait_ge(S["ar%d" % s], 16 if s == par else 12 if c == 0 else 8)
+        pe.matmul_mx(T.ps[:, 512 * c:512 * c + 2 * CAP], T.wc[:, :], T.wp[:, :], T.rc[:, 2 * CAP * c:2 * CAP * c + 2 * CAP],
+                     T.rp[:, 2 * CAP * c:2 * CAP * c + 2 * CAP], True, True).then_inc(S["pm%d" % c], 1)
+    for c in order:
+        r0 = rank_at[2 * c]
+        v.wait_ge(S["pm%d" % c], 1)
+        op(v.tensor_tensor_scan(T.z[:, 320 * c:320 * c + 320], T.msk[:, CAP * r0:CAP * r0 + 320], T.ps[:, 512 * c:512 * c + 320],
+                                NEG, A.add, A.max))
+        sync_v()
+        v.tensor_copy(T.ys[:, 16 * r0:16 * r0 + 32], T.z[:, 320 * c:320 * c + 320].indirect(T.eu[:, 8 + r0:10 + r0])).then_inc(S["yg%d" % c], 1)
+        sy.wait_ge(S["yg%d" % c], 1)
+        sy.dma_start(T.y[:, 16 * r0:16 * r0 + 32], T.ys[:, 16 * r0:16 * r0 + 32]).then_inc(S.yd, 16)
+    sy.wait_ge(S.yd, 64)
+    g.wait_ge(S.ls, sent[0])

@@ -5,27 +5,30 @@ N, CD, CAP, XC = 8, 16, 160, 1024
 XW = XC + CAP
 NEG = -5.0e29
 W = N * CD
+KP = 4 * CAP // 16
+PAR, OWN = 6, 7
 
 SCRATCH = {k: ("sbuf", [128, w], t) for t, ks in {
-    "int32": {"cd8": 8, "cdl": 32, "sl": 128, "ip": 1, "ci": 1, "ei": W, "ph": W},
-    "float32": {"row": 192, "tab": 192, "cf": 8, "kk": 24, "rst": W, "sb": W, "zz": W, "cc": W,
-                "lnf": W, "eb": W + 4, "cmpb": W + 4, "bs": W + 4, "ix": W, "jp": W, "mk": W, "gm": W, "gg": W, "hh": W,
-                "t1": W + 4, "t2": W, "raw": 16, "tin": 32, "tout": 32, "ef": 16,
-                "msk": 8 * CAP + 8, "neg": 128, "z": 8 * CAP, "ys": 128},
-    "uint16": {"cu": 8, "iu": 8, "of0": W, "of1": W, "of2": W, "of3": W, "eu": 16},
+    "int32": {"cd8": 8, "sl": 128, "ip": 1, "ci": 1, "ei": W, "ph": W},
+    "float32": {"row": 192, "tab": 128, "cf": 8, "th": 8, "thb": 8, "sb": W, "zz": 64, "cc": 96, "acc": 8, "sg": 512,
+                "lnf": W, "eng": W, "eb": W + 4, "bs0": 68, "bs1": 68, "jp": W, "mk": W, "gm": W, "gg": W, "hh": W,
+                "t10": 52, "t11": 52, "t2": 96, "tin": 32, "tout": 32,
+                "msk": 8 * CAP + 8, "neg": 128, "z": 8 * CAP + 8, "ys": 128},
+    "uint16": {"cdu": 8, "cu": 8, "iu": 8, "of0": 2 * KP, "of1": 2 * KP, "of2": 2 * KP, "of3": 2 * KP, "eu": 8},
     "bfloat16": {"xs": 4 * XW, "h": 32 * CAP, "qs": 512},
     "float8_e4m3fn_x4": {"qc": 8 * CAP, "wc": 128, "rc": 8 * CAP},
     "uint8": {"qp": 8 * CAP, "wp": 128, "rp": 8 * CAP}}.items() for k, w in ks.items()}
 SCRATCH["es"] = ("dram", [128, 1], "float32")
-SCRATCH["el"] = ("dram", [8, 128, 1], "float32")
-SCRATCH["ps"] = ("psum", [128, 4 * 512], "float32")
-SEMAPHORES = (["ldc", "ldt", "ldx", "ldq", "gi", "pb", "vt", "xgo", "vz", "ca", "cb", "est", "er", "ell", "wq", "yd", "ls", "vv", "rw",
-               "e0", "e1", "e2"]
+SCRATCH["el"] = ("dram", [8, 256, 1], "float32")
+SCRATCH["ps"] = ("psum", [128, 5 * 512], "float32")
+SEMAPHORES = (["ldc", "ldt", "ldx", "ldq", "gi", "pb", "vt", "xgo", "vz", "ca", "cb", "co", "cv", "est", "er", "ell", "wq", "yd", "ls",
+               "vv", "rw", "th", "mz"]
               + [n + str(s) for n in ("hg", "qz", "ar") for s in range(8)]
-              + [n + str(s) for n in ("pm", "yg") for s in range(4)]
-              + ["of%d%d" % (b, t) for b in (0, 1) for t in range(4)] + ["m%d_%d" % (b, k) for b in (0, 1) for k in range(3, 16)])
+              + [n + str(s) for n in ("pm", "yg") for s in range(5)] + [n + str(b) for n in ("en", "eb", "ac") for b in (0, 1)]
+              + ["of%d%d" % (b, t) for b in (0, 1) for t in range(4)]
+              + [n + str(b) for n in ("lf", "ei", "ph", "mk", "bs", "jp", "gm", "gg", "hh", "iu", "ta", "tb") for b in (0, 1)])
 
-SCALAR = [(0, 1), (0, 1, 2, 3), (0, 1, 2), (0, 1), (0, 1, 2), (0, 1), (0, 1, 2, 3), (0, 1)]
+SCALAR = [(0, 1), (0, 1, 2, 3), (0, 1, 2), (0, 1), (0, 1, 2), (0, 1), (0, 1), (0, 1, 2, 3)]
 
 
 def rank_program(g, core, T, topo):
@@ -45,19 +48,17 @@ def rank_program(g, core, T, topo):
             return 2
         return 1 if topo.same_plane(ca, cb) else 0
 
-    def chipmates(c):
-        return [r for r in range(N) if topo.chip(cores[r]) == topo.chip(c)]
+    def place(r):
+        return [k for k in range(N) if topo.chip(cores[k]) == topo.chip(cores[r])].index(r)
 
     def slot(a, b):
-        return 2 * dist(cores[a], cores[b]) + chipmates(cores[b]).index(b)
+        return 2 * dist(cores[a], cores[b]) + int(place(a) == place(b))
 
     rank_at = [None] * N
     for r in range(N):
         rank_at[slot(me, r)] = r
-    own = slot(me, me)
-    par = [s for s in (6, 7) if s != own][0]
     far_e = topo.engines(core, cores[rank_at[0]])
-    near_e = [e for e in topo.engines(core, cores[rank_at[par]]) if e not in far_e]
+    near_e = [e for e in topo.engines(core, cores[rank_at[PAR]]) if e not in far_e]
 
     def msk(es):
         m = 0
@@ -65,15 +66,15 @@ def rank_program(g, core, T, topo):
             m |= 1 << e
         return int(m)
 
+    def dst_id(s):
+        rid, pid, _ = topo.addr(cores[rank_at[s]])
+        return DstId(rid=rid, pnc=pid)
+
     sent = [0]
 
     def tr(s, es, sem, src, dst):
-        rid, pid, _ = topo.addr(cores[rank_at[s]])
         sent[0] += len(es)
-        return RemoteDMATransfer(dst_ids=[DstId(rid=rid, pnc=pid)], dma_engine_mask=msk(es), remote_sem=S[sem], src=src, dst=dst)
-
-    def there(s):
-        return slot(rank_at[s], me)
+        return RemoteDMATransfer(dst_ids=[dst_id(s)], dma_engine_mask=msk(es), remote_sem=S[sem], src=src, dst=dst)
 
     for k in range(8):
         (sy if k % 2 == 0 else sc).dma_start(T.cd8[16 * k:16 * k + 16, :], T.cd[:, :]).then_inc(S.ldc, 16)
@@ -81,6 +82,8 @@ def rank_program(g, core, T, topo):
     sc.dma_start(T.sl[0:1, 64:128], T.ln[:, :]).then_inc(S.ldt, 16)
     sy.dma_start(T.xs[:, 0:1024], T.x[:, 0:1024]).then_inc(S.ldx, 16)
     sc.dma_start(T.xs[:, 1024:2048], T.x[:, 1024:2048]).then_inc(S.ldx, 16)
+    sy.wait_ge(S.cv, 1)
+    sy.dma_start(T.cu[:, OWN:OWN + 1], T.cdu[:, me:me + 1]).then_inc(S.co, 16)
     sy.wait_ge(S.xgo, 1)
     sy.dma_start(T.xs[:, 2048:3072], T.x[:, 2048:3072]).then_inc(S.ldx, 16)
     sc.wait_ge(S.xgo, 1)
@@ -88,19 +91,19 @@ def rank_program(g, core, T, topo):
     sc.dma_start(T.qs[:, :], T.qw[:, :]).then_inc(S.ldq, 16)
 
     g.iota(T.ip[:, 0:1], [[0, 1]], 0, 1).then_inc(S.gi, 1)
-    for out, pat, base in ((T.kk[:, 0:8], [[CAP, 8]], 0), (T.kk[:, 8:16], [[0, 4], [CAP, 2]], -1), (T.kk[:, 16:24], [[0, 2], [CD, 4]], 0),
-                           (T.cc[:, :], [[0, 8], [16, 16]], -16)):
+    for out, pat, base in ((T.th[:, :], [[16 * KP, 2], [256, 4]], 0), (T.sb[:, :], [[CAP, 8], [0, CD]], 0),
+                           (T.cc[:, :], [[16 * KP, 2], [16, 48]], -16)):
         g.iota(out, pat, base, 0, allow_small_or_imprecise_dtypes=True).then_inc(S.gi, 1)
-    g.wait_ge(S.ldc, 128)
+    g.wait_ge(S.cv, 1)
 
     def cdt(s, es, sem):
-        r, d = rank_at[s], there(s)
-        return tr(s, es, sem, T.cd8[:, r:r + 1], T.cdl[:, 4 * d:4 * d + 1])
+        r = rank_at[s]
+        return tr(s, es, sem, T.cdu[:, r:r + 1], T.cu[:, s:s + 1])
     g.remote_dma_fused([cdt(s, far_e[2 * s:2 * s + 2], "ca") for s in range(4)], local_sem=S.ls)
-    g.remote_dma_fused([cdt(4, far_e[0:4], "cb"), cdt(5, far_e[4:8], "cb"), cdt(par, near_e[0:4], "cb")], local_sem=S.ls)
+    g.remote_dma_fused([cdt(4, far_e[0:4], "cb"), cdt(5, far_e[4:8], "cb"), cdt(PAR, near_e[0:4], "cb")], local_sem=S.ls)
     g.sem_inc(S.xgo, 1)
     g.wait_ge(S.vt, 1)
-    g.partition_broadcast(T.tab[:, 0:192], T.row[0:1, 0:192], 128).then_inc(S.pb, 1)
+    g.partition_broadcast(T.tab[:, :], T.row[0:1, 64:192], 128).then_inc(S.pb, 1)
 
     n = {"vv": 0}
 
@@ -112,203 +115,200 @@ def rank_program(g, core, T, topo):
         v.wait_ge(S.vv, n["vv"])
 
     v.memset(T.xs[:, 4 * XC:4 * XW], 0.0).then_inc(S.vz, 1)
-    v.memset(T.raw[:, :], 0.0).then_inc(S.rw, 1)
+    v.memset(T.tin[:, :], 0.0).then_inc(S.rw, 1)
     op(v.memset(T.zz[:, :], 0.0))
-    op(v.memset(T.sb[:, :], 0.0))
-    op(v.memset(T.rst[:, :], 1.0))
-    for b in ("eb", "cmpb", "bs", "t1"):
-        op(v.memset(T[b][:, 0:1], 0.0))
-    v.wait_ge(S.gi, 5)
-    op(v.tensor_scalar(T.ci[:, 0:1], T.ip[:, 0:1], 15, None, A.bitwise_and))
-    sync_v()
-    op(v.tensor_copy(T.cf[:, 0:1], T.ci[:, 0:1]))
-    op(v.tensor_copy(T.rst[:, 0:W:CD], T.zz[:, 0:8]))
-    op(v.tensor_copy(T.sb[:, 0:W:CD], T.kk[:, 16:24]))
-    sync_v()
-    op(v.tensor_scalar(T.cf[:, 1:2], T.cf[:, 0:1], 16.0, -16.0, A.mult, A.add))
-    for t in range(4):
-        op(v.tensor_scalar(T.cf[:, 2 + t:3 + t], T.cf[:, 0:1], 4.0, float(t), A.mult, A.add))
+    op(v.memset(T.neg[:, :], NEG))
+    for b, c in (("z", 0), ("eb", 0), ("bs0", 0), ("bs1", 0), ("t10", 48), ("t11", 48)):
+        op(v.memset(T[b][:, c:c + 1], 0.0))
+    v.wait_ge(S.ldc, 128)
+    v.tensor_copy(T.cdu[:, :], T.cd8[:, :]).then_inc(S.cv, 1)
     v.wait_ge(S.ldt, 32)
     for k in range(4):
         op(v.tensor_copy(T.row[0:1, 16 * k:16 * k + 16], T.sl[0:1, k:64:4]))
         op(v.tensor_copy(T.row[0:1, 64 + 16 * k:80 + 16 * k], T.sl[0:1, 64 + k:128:4]))
+    v.wait_ge(S.gi, 4)
+    op(v.tensor_scalar(T.ci[:, 0:1], T.ip[:, 0:1], 15, None, A.bitwise_and))
     sync_v()
     v.tensor_tensor(T.row[0:1, 128:192], T.row[0:1, 0:64], T.row[0:1, 64:128], A.add).then_inc(S.vt, 1)
-    v.wait_ge(S.ldc, 128)
-    op(v.tensor_copy(T.cdl[:, 4 * own:4 * own + 1], T.cd8[:, me:me + 1]))
-    op(v.memset(T.neg[:, :], NEG))
+    op(v.tensor_copy(T.cf[:, 0:1], T.ci[:, 0:1]))
     op(v.memset(T.msk[:, :], 0.0))
     sync_v()
-    op(v.tensor_copy(T.msk[:, 0:8 * CAP:CAP], T.neg[:, 0:8]))
+    op(v.tensor_scalar(T.cf[:, 1:2], T.cf[:, 0:1], 16.0, -0.5, A.mult, A.add))
+    for t in range(4):
+        op(v.tensor_scalar(T.cf[:, 2 + t:3 + t], T.cf[:, 0:1], 4.0, float(t), A.mult, A.add))
+    v.tensor_copy(T.msk[:, 0:8 * CAP:CAP], T.neg[:, 0:8]).then_inc(S.mz, 1)
     sync_v()
+    v.tensor_scalar(T.thb[:, :], T.th[:, :], T.cf[:, 1:2], None, A.add).then_inc(S.th, 1)
 
-    v.wait_ge(S.ca, 8)
-    v.wait_ge(S.cb, 12)
-    v.tensor_copy(T.cu[:, 0:8], T.cdl[:, 0:32:4]).then_inc(S.e0, 1)
-    v.wait_ge(S.pb, 1)
-    v.wait_ge(S.e0, 1)
-    v.tensor_copy(T.lnf[:, :], T.tab[:, 64:128].indirect(T.cu[:, 0:8])).then_inc(S.e1, 1)
-    v.wait_ge(S.e1, 1)
-    v.tensor_tensor_scan(T.eb[:, 1:W + 1], T.rst[:, :], T.lnf[:, :], 0.0, A.mult, A.add).then_inc(S.e2, 1)
-    v.wait_ge(S.e2, 1)
+    def counts(b):
+        sc.wait_ge(S["eb%d" % b], 1)
+        for m in range(3):
+            c = 4 * b + m
+            sc.activation(T.sg[:, 64 * c:64 * c + 63], T.eb[:, 64 * b + 1:64 * b + 64], F.Sign, bias=T.thb[:, c:c + 1], scale=-1.0,
+                          accum_out=T.acc[:, c:c + 1]).then_inc(S["ac%d" % b], 1)
 
-    def lists(b, between=None):
-        lo, hi, c0, c1 = 64 * b, 64 * b + 64, 4 * b, 4 * b + 4
+    sc.wait_ge(S.pb, 1)
+    sc.wait_ge(S.th, 1)
+    sc.wait_ge(S.ca, 8)
+    sc.activation(T.eng[:, 0:64], T.tab[:, 64:128].indirect(T.cu[:, 0:4]), F.Copy).then_inc(S.en0, 1)
+    counts(0)
+    sc.wait_ge(S.cb, 12)
+    sc.wait_ge(S.co, 16)
+    sc.activation(T.lnf[:, 64:128], T.tab[:, 0:64].indirect(T.cu[:, 4:8]), F.Copy).then_inc(S.lf1, 1)
+    sc.activation(T.eng[:, 64:128], T.tab[:, 64:128].indirect(T.cu[:, 4:8]), F.Copy).then_inc(S.en1, 1)
+    counts(1)
+
+    def ends(b):
+        lo, hi = 64 * b, 64 * b + 64
+        v.wait_ge(S["lf%d" % b], 1)
+        v.tensor_tensor_scan(T.eb[:, lo + 1:hi + 1], T.sb[:, lo:hi], T.lnf[:, lo:hi], 0.0, A.max, A.add).then_inc(S["eb%d" % b], 1)
+
+    def lists(b, between):
+        lo, hi, c0 = 64 * b, 64 * b + 64, 4 * b
+        bs, t1 = T["bs%d" % b], T["t1%d" % b]
 
         def m(k, ins):
-            ins.then_inc(S["m%d_%d" % (b, k)], 1)
+            ins.then_inc(S[k + str(b)], 1)
 
         def wm(*ks):
             for k in ks:
-                v.wait_ge(S["m%d_%d" % (b, k)], 1)
+                v.wait_ge(S[k + str(b)], 3 if k == "ac" else 1)
 
-        m(3, v.tensor_copy(T.ei[:, lo:hi], T.eb[:, lo:hi]))
-        m(4, v.tensor_scalar(T.cmpb[:, lo + 1:hi + 1], T.eb[:, lo + 1:hi + 1], T.cf[:, 1:2], None, A.is_lt))
-        m(5, v.tensor_tensor(T.bs[:, lo + 1:hi + 1], T.tab[:, 128:192].indirect(T.cu[:, c0:c1]), T.eb[:, lo + 1:hi + 1], A.subtract))
-        wm(3)
-        m(6, v.tensor_scalar(T.ph[:, lo:hi], T.ei[:, lo:hi], 15, None, A.bitwise_and))
-        wm(4)
-        m(7, v.tensor_tensor_scan(T.ix[:, lo:hi], T.cmpb[:, lo:hi], T.sb[:, lo:hi], -1.0, A.add, A.max))
-        wm(5)
-        m(8, v.tensor_tensor(T.jp[:, lo:hi], T.bs[:, lo + 1:hi + 1], T.bs[:, lo:hi], A.subtract))
-        wm(6)
-        m(9, v.tensor_scalar(T.mk[:, lo:hi], T.ph[:, lo:hi], T.cf[:, 0:1], None, A.is_le))
-        wm(7)
-        m(10, v.tensor_copy(T.iu[:, c0:c1], T.ix[:, lo + CD - 1:hi:CD]))
-        wm(8, 9)
-        m(11, v.tensor_tensor(T.gm[:, lo:hi], T.jp[:, lo:hi], T.mk[:, lo:hi], A.mult))
-        wm(11)
-        m(12, v.tensor_tensor_scan(T.gg[:, lo:hi], T.zz[:, lo:hi], T.gm[:, lo:hi], 0.0, A.add, A.add))
-        wm(12)
-        m(13, v.tensor_tensor(T.hh[:, lo:hi], T.bs[:, lo + 1:hi + 1], T.gg[:, lo:hi], A.subtract))
-        if between is not None:
-            between()
-        wm(10, 13)
-        m(14, v.tensor_tensor(T.t1[:, lo + 1:hi + 1], T.hh[:, lo:hi].indirect(T.iu[:, c0:c1]), T.cc[:, lo:hi], A.add))
-        wm(14)
-        m(15, v.tensor_tensor(T.t2[:, lo:hi], T.gg[:, lo:hi].indirect(T.iu[:, c0:c1]), T.t1[:, lo:hi], A.add))
-        wm(15)
+        wm("eb")
+        m("ei", v.tensor_copy(T.ei[:, lo:hi], T.eb[:, lo:hi]))
+        wm("en")
+        m("bs", v.tensor_tensor(bs[:, 1:65], T.eng[:, lo:hi], T.eb[:, lo + 1:hi + 1], A.subtract))
+        wm("ei")
+        m("ph", v.tensor_scalar(T.ph[:, lo:hi], T.ei[:, lo:hi], 15, None, A.bitwise_and))
+        wm("bs")
+        m("jp", v.tensor_tensor(T.jp[:, lo:hi], bs[:, 1:65], bs[:, 0:64], A.subtract))
+        wm("ph")
+        m("mk", v.tensor_scalar(T.mk[:, lo:hi], T.ph[:, lo:hi], T.cf[:, 0:1], None, A.is_le))
+        wm("ac")
+        m("iu", v.tensor_scalar(T.iu[:, c0:c0 + 3], T.acc[:, c0:c0 + 3], 0.5, 31.5, A.mult, A.add))
+        wm("jp", "mk")
+        m("gm", v.tensor_tensor(T.gm[:, lo:hi], T.jp[:, lo:hi], T.mk[:, lo:hi], A.mult))
+        between()
+        wm("gm")
+        m("gg", v.tensor_tensor_scan(T.gg[:, lo:hi], T.zz[:, :], T.gm[:, lo:hi], 0.0, A.add, A.add))
+        m("hh", v.tensor_tensor_scan(T.hh[:, lo:hi], T.jp[:, lo:hi], T.gm[:, lo:hi], 0.0, A.add, A.subtract))
+        wm("iu", "gg")
+        m("ta", v.tensor_tensor(t1[:, 0:48], T.gg[:, lo:hi].indirect(T.iu[:, c0:c0 + 3]), T.cc[:, 48 * b:48 * b + 48], A.add))
+        wm("ta", "hh")
+        m("tb", v.tensor_tensor(T.t2[:, 48 * b:48 * b + 48], T.hh[:, lo:hi].indirect(T.iu[:, c0:c0 + 3]), t1[:, 1:49], A.add))
+        wm("tb")
         for t in range(4):
-            v.tensor_scalar(T["of%d" % t][:, lo:hi], T.t2[:, lo:hi], 4.0, T.cf[:, 2 + t:3 + t], A.mult, A.add).then_inc(S["of%d%d" % (b, t)], 1)
+            v.tensor_scalar(T["of%d" % t][:, KP * b:KP * b + KP], T.t2[:, 48 * b:48 * b + KP], 4.0, T.cf[:, 2 + t:3 + t],
+                            A.mult, A.add).then_inc(S["of%d%d" % (b, t)], 1)
 
     seen = {"s": [], "v": []}
 
-    def gather(key, s):
+    def gather(key, s, t):
         q = sc if key == "s" else v
-        role = 6 if s == own else 7 if s == par else s
-        for t in range(4):
-            if (t in SCALAR[role]) != (key == "s"):
-                continue
-            if not seen[key]:
-                q.wait_ge(S.ldx, 64)
-                q.wait_ge(S.vz, 1)
-            sem = "of%d%d" % (s // 4, t)
-            if sem not in seen[key]:
-                q.wait_ge(S[sem], 1)
-                seen[key].append(sem)
-            out, win = T.h[:, 640 * s + t:640 * s + 640:4], T.xs[:, 0:4 * XW].indirect(T["of%d" % t][:, CD * s + 2:CD * s + 12])
-            ins = sc.activation(out, win, F.Copy) if key == "s" else v.tensor_copy(out, win)
-            ins.then_inc(S["hg%d" % s], 1)
+        if not seen[key]:
+            q.wait_ge(S.ldx, 64)
+            q.wait_ge(S.vz, 1)
+        sem = "of%d%d" % (s // 4, t)
+        if sem not in seen[key]:
+            q.wait_ge(S[sem], 1)
+            seen[key].append(sem)
+        out, win = T.h[:, 640 * s + t:640 * s + 640:4], T.xs[:, 0:4 * XW].indirect(T["of%d" % t][:, 10 * s:10 * s + 10])
+        ins = sc.activation(out, win, F.Copy) if key == "s" else v.tensor_copy(out, win)
+        ins.then_inc(S["hg%d" % s], 1)
 
     def quant(s):
         v.wait_ge(S["hg%d" % s], 4)
-        cc, pp = (T.rc, T.rp) if s == own else (T.qc, T.qp)
+        cc, pp = (T.rc, T.rp) if s == OWN else (T.qc, T.qp)
         v.quantize_mx(cc[:, CAP * s:CAP * s + CAP], pp[:, CAP * s:CAP * s + CAP], T.h[:, 640 * s:640 * s + 640]).then_inc(S["qz%d" % s], 1)
 
-    for s in (0, 1, 2, 3, 4, 5, par, own):
-        gather("s", s)
+    for s in range(8):
+        for t in SCALAR[s]:
+            gather("s", s, t)
 
-    lists(0)
-    gather("v", 0)
+    v.wait_ge(S.pb, 1)
+    v.wait_ge(S.ca, 8)
+    v.tensor_copy(T.lnf[:, 0:64], T.tab[:, 0:64].indirect(T.cu[:, 0:4])).then_inc(S.lf0, 1)
+    ends(0)
+    lists(0, lambda: ends(1))
+    gather("v", 0, 2)
+    gather("v", 0, 3)
     quant(0)
-    gather("v", 1)
     lists(1, lambda: quant(1))
     for s in (2, 4):
-        gather("v", s)
-        gather("v", s + 1)
+        gather("v", s, 3)
+        gather("v", s + 1, 3)
         quant(s)
+        gather("v", s + 1, 2)
         quant(s + 1)
-    gather("v", par)
+    gather("v", PAR, 2)
+    gather("v", PAR, 3)
+    quant(PAR)
     v.wait_ge(S.ldq, 16)
     v.quantize_mx(T.wc[:, :], T.wp[:, :], T.qs[:, :]).then_inc(S.wq, 1)
-    quant(par)
-    gather("v", own)
 
-    sy.wait_ge(S.e2, 1)
-    for d in range(4):
-        e0 = CD * rank_at[2 * d]
-        sy.dma_start(T.es[e0:e0 + 32, :], T.eb[0:1, 32 * d + 1:32 * d + 33]).then_inc(S.est, 16)
-    sy.dma_start(T.el[me, CD * me:CD * me + CD, :], T.eb[0:1, CD * own + 1:CD * own + CD + 1]).then_inc(S.est, 16)
+    sy.wait_ge(S.eb0, 1)
+    sy.wait_ge(S.eb1, 1)
+    sy.dma_start(T.es[:, :], T.eb[0:1, 1:W + 1]).then_inc(S.est, 16)
+    sy.dma_start(T.el[me, W:W + CD, :], T.eb[0:1, CD * OWN + 1:CD * OWN + CD + 1]).then_inc(S.est, 16)
 
-    g.wait_ge(S.est, 80)
-    ids = []
-    for s in [0, 1, 2, 3, 4, 5, par]:
-        rid, pid, _ = topo.addr(cores[rank_at[s]])
-        ids.append(DstId(rid=rid, pnc=pid))
-    g.remote_dma_fused([RemoteDMATransfer(dst_ids=ids, dma_engine_mask=msk(far_e[0:1]), remote_sem=S.er, srcs=[T.es[:, :]],
-                                          dsts=[T.el[me] for _ in ids])], local_sem=S.ls)
+    g.wait_ge(S.est, 32)
+    g.remote_dma_fused([RemoteDMATransfer(dst_ids=[dst_id(s) for s in range(7)], dma_engine_mask=msk(far_e[0:1]), remote_sem=S.er,
+                                          srcs=[T.es[:, :]], dsts=[T.el[me, W - CD * s:2 * W - CD * s, :] for s in range(7)])],
+                       local_sem=S.ls)
     sent[0] += 1
 
     def codes(s, es):
-        d = there(s)
-        return tr(s, es, "ar%d" % d, T.qc[:, CAP * s:CAP * s + CAP].bitcast(dt.uint8), T.rc[:, CAP * d:CAP * d + CAP].bitcast(dt.uint8))
+        return tr(s, es, "ar%d" % s, T.qc[:, CAP * s:CAP * s + CAP].bitcast(dt.uint8), T.rc[:, CAP * s:CAP * s + CAP].bitcast(dt.uint8))
 
     def plane(s, es):
-        d = there(s)
-        return tr(s, es, "ar%d" % d, T.qp[:, CAP * s:CAP * s + CAP], T.rp[:, CAP * d:CAP * d + CAP])
+        return tr(s, es, "ar%d" % s, T.qp[:, CAP * s:CAP * s + CAP], T.rp[:, CAP * s:CAP * s + CAP])
 
-    for s in (0, 2, 4):
+    for s in range(6):
         g.wait_ge(S["qz%d" % s], 1)
-        if s == 0:
-            g.remote_dma_fused([codes(0, far_e)], local_sem=S.ls)
-            g.wait_ge(S.qz1, 1)
-            g.remote_dma_fused([codes(1, far_e)], local_sem=S.ls)
-        else:
-            g.wait_ge(S["qz%d" % (s + 1)], 1)
-            g.remote_dma_fused([codes(s, far_e[0:4]), codes(s + 1, far_e[4:8])], local_sem=S.ls)
-        g.remote_dma_fused([plane(s, far_e[0:4]), plane(s + 1, far_e[4:8])], local_sem=S.ls)
-    g.wait_ge(S["qz%d" % par], 1)
-    g.remote_dma_fused([codes(par, near_e)], local_sem=S.ls)
-    g.remote_dma_fused([plane(par, near_e)], local_sem=S.ls)
+        g.remote_dma_fused([codes(s, far_e)], local_sem=S.ls)
+        if s % 2:
+            g.remote_dma_fused([plane(s - 1, far_e[0:4]), plane(s, far_e[4:8])], local_sem=S.ls)
+    g.wait_ge(S["qz%d" % PAR], 1)
+    g.remote_dma_fused([codes(PAR, near_e)], local_sem=S.ls)
+    g.remote_dma_fused([plane(PAR, near_e)], local_sem=S.ls)
 
-    sy.wait_ge(S.est, 80)
+    sy.wait_ge(S.est, 32)
     sy.wait_ge(S.er, 7)
     sy.wait_ge(S.rw, 1)
     for a in range(4):
-        sy.dma_start(T.raw[32 * a:32 * a + 8, :], T.el[:, CD * me:CD * me + CD, :]).then_inc(S.ell, 16)
-    v.wait_ge(S.ell, 64)
-    op(v.tensor_copy(T.tin[:, 0:16], T.raw[:, :]))
-    op(v.tensor_copy(T.tin[:, 16:32], T.raw[:, :]))
-    sync_v()
+        for c in (0, CD):
+            sy.dma_start(T.tin[32 * a:32 * a + 8, c:c + CD], T.el[:, W:W + CD, :]).then_inc(S.ell, 16)
+    v.wait_ge(S.ell, 128)
     op(v.transpose(T.tout[:, :], T.tin[:, :]))
     sync_v()
-    op(v.tensor_tensor(T.ef[:, 0:8], T.tout[:, 0:8], T.kk[:, 0:8], A.add))
-    op(v.tensor_tensor(T.ef[:, 8:16], T.tout[:, 0:8], T.kk[:, 8:16], A.add))
+    op(v.tensor_copy(T.eu[:, :], T.tout[:, 0:8]))
+    v.wait_ge(S.mz, 1)
     sync_v()
-    op(v.tensor_copy(T.eu[:, :], T.ef[:, :]))
-    sync_v()
-    op(v.tensor_copy(T.msk[:, :].indirect(T.eu[:, 0:8]), T.neg[:, :]))
-    quant(own)
+    op(v.tensor_copy(T.msk[:, :].indirect(T.eu[:, :]), T.neg[:, :]))
     sync_v()
 
+    units = [(0, 2), (2, 2), (4, 2), (OWN, 1), (PAR, 1)]
     pe.wait_ge(S.wq, 1)
-    order = [0, 1, 3, 2]
-    for c in order:
-        for s in (2 * c, 2 * c + 1):
-            if s == own:
-                pe.wait_ge(S["qz%d" % own], 1)
+    for u, (s0, k) in enumerate(units):
+        for s in range(s0, s0 + k):
+            if s == OWN:
+                pe.wait_ge(S["qz%d" % s], 1)
             else:
-                pe.wait_ge(S["ar%d" % s], 16 if s == par else 12 if c == 0 else 8)
-        pe.matmul_mx(T.ps[:, 512 * c:512 * c + 2 * CAP], T.wc[:, :], T.wp[:, :], T.rc[:, 2 * CAP * c:2 * CAP * c + 2 * CAP],
-                     T.rp[:, 2 * CAP * c:2 * CAP * c + 2 * CAP], True, True).then_inc(S["pm%d" % c], 1)
-    for c in order:
-        r0 = rank_at[2 * c]
-        v.wait_ge(S["pm%d" % c], 1)
-        op(v.tensor_tensor_scan(T.z[:, 320 * c:320 * c + 320], T.msk[:, CAP * r0:CAP * r0 + 320], T.ps[:, 512 * c:512 * c + 320],
-                                NEG, A.add, A.max))
+                pe.wait_ge(S["ar%d" % s], 16 if s == PAR else 12)
+        a, b = CAP * s0, CAP * (s0 + k)
+        pe.matmul_mx(T.ps[:, 512 * u:512 * u + b - a], T.wc[:, :], T.wp[:, :], T.rc[:, a:b], T.rp[:, a:b], True, True).then_inc(S["pm%d" % u], 1)
+    for u, (s0, k) in enumerate(units):
+        a, b = CAP * s0, CAP * (s0 + k)
+        v.wait_ge(S["pm%d" % u], 1)
+        op(v.tensor_tensor_scan(T.z[:, a + 1:b + 1], T.msk[:, a:b], T.ps[:, 512 * u:512 * u + b - a], NEG, A.add, A.max))
+        if u == 0:
+            quant(OWN)
+        if s0 == OWN:
+            continue
+        r0 = min(rank_at[s0], rank_at[s0 + 1])
         sync_v()
-        v.tensor_copy(T.ys[:, 16 * r0:16 * r0 + 32], T.z[:, 320 * c:320 * c + 320].indirect(T.eu[:, 8 + r0:10 + r0])).then_inc(S["yg%d" % c], 1)
-        sy.wait_ge(S["yg%d" % c], 1)
+        v.tensor_copy(T.ys[:, 16 * r0:16 * r0 + 32], T.z[:, 0:a + 2 * CAP + 1].indirect(T.eu[:, r0:r0 + 2])).then_inc(S["yg%d" % u], 1)
+        sy.wait_ge(S["yg%d" % u], 1)
         sy.dma_start(T.y[:, 16 * r0:16 * r0 + 32], T.ys[:, 16 * r0:16 * r0 + 32]).then_inc(S.yd, 16)
     sy.wait_ge(S.yd, 64)
     g.wait_ge(S.ls, sent[0])

@@ -7,28 +7,31 @@ NEG = -5.0e29
 W = N * CD
 KP = 4 * CAP // 16
 PAR, OWN = 6, 7
+SLOT = [(0, 1), (2, 4), (3, 5), (PAR, OWN)]
+UNITS = [(0, 2), (2, 2), (OWN, 1), (4, 1), (5, 1), (PAR, 1)]
+
+VECTOR = ("lf0 eb0 ei0 bs0 ph0 jp0 mk0 iu0 eb1 gm0 ei1 bs1 gg0 hh0 ph1 ta0 jp1 tb0 mk1 iu1 o00 o01 o02 o03 gm1 "
+          "g02 gg1 hh1 g03 ta1 q0 tb1 g13 o10 o11 o12 o13 q1 g23 g33 q2 g32 g43 q3 g42 g53 q4 g63 q5 g62 wq q6 "
+          "tr g73 eu sc q7 z0 z1 z2 z3 z4 z5 y3")
+SCALAR = ("en0 ac0 lf1 en1 ac1 g00 g01 g10 g11 g12 g20 g21 g22 g30 g31 g40 g41 g50 g51 g52 g60 g61 "
+          "g70 g71 g72 y0 y1 y2")
 
 SCRATCH = {k: ("sbuf", [128, w], t) for t, ks in {
     "int32": {"cd8": 8, "sl": 128, "ip": 1, "ci": 1, "ei": W, "ph": W},
     "float32": {"row": 192, "tab": 128, "cf": 8, "th": 8, "thb": 8, "sb": W, "zz": 64, "cc": 96, "acc": 8, "sg": 512,
                 "lnf": W, "eng": W, "eb": W + 4, "bs0": 68, "bs1": 68, "jp": W, "mk": W, "gm": W, "gg": W, "hh": W,
-                "t10": 52, "t11": 52, "t2": 96, "tin": 32, "tout": 32,
-                "msk": 8 * CAP + 8, "neg": 128, "z": 8 * CAP + 8, "ys": 128},
+                "t10": 52, "t11": 52, "t2": 96, "tin": 32, "tout": 32, "z": 8 * CAP + 8, "ys": 128},
     "uint16": {"cdu": 8, "cu": 8, "iu": 8, "of0": 2 * KP, "of1": 2 * KP, "of2": 2 * KP, "of3": 2 * KP, "eu": 8},
-    "bfloat16": {"xs": 4 * XW, "h": 32 * CAP, "qs": 512},
+    "bfloat16": {"xs": 4 * XW, "h": 32 * CAP, "qs": 512, "msk": 8 * CAP + 8, "neg": 128},
     "float8_e4m3fn_x4": {"qc": 8 * CAP, "wc": 128, "rc": 8 * CAP},
     "uint8": {"qp": 8 * CAP, "wp": 128, "rp": 8 * CAP}}.items() for k, w in ks.items()}
 SCRATCH["es"] = ("dram", [128, 1], "float32")
 SCRATCH["el"] = ("dram", [8, 256, 1], "float32")
-SCRATCH["ps"] = ("psum", [128, 5 * 512], "float32")
-SEMAPHORES = (["ldc", "ldt", "ldx", "ldq", "gi", "pb", "vt", "xgo", "vz", "ca", "cb", "co", "cv", "est", "er", "ell", "wq", "yd", "ls",
-               "vv", "rw", "th", "mz"]
-              + [n + str(s) for n in ("hg", "qz", "ar") for s in range(8)]
-              + [n + str(s) for n in ("pm", "yg") for s in range(5)] + [n + str(b) for n in ("en", "eb", "ac") for b in (0, 1)]
-              + ["of%d%d" % (b, t) for b in (0, 1) for t in range(4)]
-              + [n + str(b) for n in ("lf", "ei", "ph", "mk", "bs", "jp", "gm", "gg", "hh", "iu", "ta", "tb") for b in (0, 1)])
-
-SCALAR = [(0, 1), (0, 1, 2, 3), (0, 1, 2), (0, 1), (0, 1, 2), (0, 1), (0, 1), (0, 1, 2, 3)]
+SCRATCH["ps"] = ("psum", [128, len(UNITS) * 512], "float32")
+SEMAPHORES = (["ldc", "ldt", "ldx", "ldq", "gi", "pl", "pe", "vt", "vl", "xgo", "vz", "ca", "cb", "co", "cv", "est", "er", "ell", "yd", "ls",
+               "vv", "th", "mz", "rw"]
+              + ["hg%d" % s for s in range(8)] + ["ar%d" % s for s in range(7)] + ["pm%d" % u for u in range(len(UNITS))]
+              + [k for k in (VECTOR + " " + SCALAR).split() if k[0] != "g" or k[1] in "gm"])
 
 
 def rank_program(g, core, T, topo):
@@ -52,7 +55,7 @@ def rank_program(g, core, T, topo):
         return [k for k in range(N) if topo.chip(cores[k]) == topo.chip(cores[r])].index(r)
 
     def slot(a, b):
-        return 2 * dist(cores[a], cores[b]) + int(place(a) == place(b))
+        return SLOT[dist(cores[a], cores[b])][int(place(a) == place(b))]
 
     rank_at = [None] * N
     for r in range(N):
@@ -102,8 +105,10 @@ def rank_program(g, core, T, topo):
     g.remote_dma_fused([cdt(s, far_e[2 * s:2 * s + 2], "ca") for s in range(4)], local_sem=S.ls)
     g.remote_dma_fused([cdt(4, far_e[0:4], "cb"), cdt(5, far_e[4:8], "cb"), cdt(PAR, near_e[0:4], "cb")], local_sem=S.ls)
     g.sem_inc(S.xgo, 1)
+    g.wait_ge(S.vl, 4)
+    g.partition_broadcast(T.tab[:, 0:64], T.row[0:1, 64:128], 128).then_inc(S.pl, 1)
     g.wait_ge(S.vt, 1)
-    g.partition_broadcast(T.tab[:, :], T.row[0:1, 64:192], 128).then_inc(S.pb, 1)
+    g.partition_broadcast(T.tab[:, 64:128], T.row[0:1, 128:192], 128).then_inc(S.pe, 1)
 
     n = {"vv": 0}
 
@@ -114,7 +119,6 @@ def rank_program(g, core, T, topo):
     def sync_v():
         v.wait_ge(S.vv, n["vv"])
 
-    v.memset(T.xs[:, 4 * XC:4 * XW], 0.0).then_inc(S.vz, 1)
     v.memset(T.tin[:, :], 0.0).then_inc(S.rw, 1)
     op(v.memset(T.zz[:, :], 0.0))
     op(v.memset(T.neg[:, :], NEG))
@@ -122,13 +126,16 @@ def rank_program(g, core, T, topo):
         op(v.memset(T[b][:, c:c + 1], 0.0))
     v.wait_ge(S.ldc, 128)
     v.tensor_copy(T.cdu[:, :], T.cd8[:, :]).then_inc(S.cv, 1)
-    v.wait_ge(S.ldt, 32)
-    for k in range(4):
-        op(v.tensor_copy(T.row[0:1, 16 * k:16 * k + 16], T.sl[0:1, k:64:4]))
-        op(v.tensor_copy(T.row[0:1, 64 + 16 * k:80 + 16 * k], T.sl[0:1, 64 + k:128:4]))
     v.wait_ge(S.gi, 4)
     op(v.tensor_scalar(T.ci[:, 0:1], T.ip[:, 0:1], 15, None, A.bitwise_and))
+    v.wait_ge(S.ldt, 32)
+    for k in range(4):
+        v.tensor_copy(T.row[0:1, 64 + 16 * k:80 + 16 * k], T.sl[0:1, 64 + k:128:4]).then_inc(S.vl, 1)
+    for k in range(4):
+        op(v.tensor_copy(T.row[0:1, 16 * k:16 * k + 16], T.sl[0:1, k:64:4]))
+    v.memset(T.xs[:, 4 * XC:4 * XW], 0.0).then_inc(S.vz, 1)
     sync_v()
+    v.wait_ge(S.vl, 4)
     v.tensor_tensor(T.row[0:1, 128:192], T.row[0:1, 0:64], T.row[0:1, 64:128], A.add).then_inc(S.vt, 1)
     op(v.tensor_copy(T.cf[:, 0:1], T.ci[:, 0:1]))
     op(v.memset(T.msk[:, :], 0.0))
@@ -140,121 +147,91 @@ def rank_program(g, core, T, topo):
     sync_v()
     v.tensor_scalar(T.thb[:, :], T.th[:, :], T.cf[:, 1:2], None, A.add).then_inc(S.th, 1)
 
-    def counts(b):
-        sc.wait_ge(S["eb%d" % b], 1)
-        for m in range(3):
-            c = 4 * b + m
-            sc.activation(T.sg[:, 64 * c:64 * c + 63], T.eb[:, 64 * b + 1:64 * b + 64], F.Sign, bias=T.thb[:, c:c + 1], scale=-1.0,
-                          accum_out=T.acc[:, c:c + 1]).then_inc(S["ac%d" % b], 1)
+    def pick(q, out, win):
+        return v.tensor_copy(out, win) if q is v else sc.activation(out, win, F.Copy)
 
-    sc.wait_ge(S.pb, 1)
-    sc.wait_ge(S.th, 1)
-    sc.wait_ge(S.ca, 8)
-    sc.activation(T.eng[:, 0:64], T.tab[:, 64:128].indirect(T.cu[:, 0:4]), F.Copy).then_inc(S.en0, 1)
-    counts(0)
-    sc.wait_ge(S.cb, 12)
-    sc.wait_ge(S.co, 16)
-    sc.activation(T.lnf[:, 64:128], T.tab[:, 0:64].indirect(T.cu[:, 4:8]), F.Copy).then_inc(S.lf1, 1)
-    sc.activation(T.eng[:, 64:128], T.tab[:, 64:128].indirect(T.cu[:, 4:8]), F.Copy).then_inc(S.en1, 1)
-    counts(1)
-
-    def ends(b):
-        lo, hi = 64 * b, 64 * b + 64
-        v.wait_ge(S["lf%d" % b], 1)
-        v.tensor_tensor_scan(T.eb[:, lo + 1:hi + 1], T.sb[:, lo:hi], T.lnf[:, lo:hi], 0.0, A.max, A.add).then_inc(S["eb%d" % b], 1)
-
-    def lists(b, between):
+    def pass_step(q, k, b):
         lo, hi, c0 = 64 * b, 64 * b + 64, 4 * b
-        bs, t1 = T["bs%d" % b], T["t1%d" % b]
+        bs, t1, cu, iu = T["bs%d" % b], T["t1%d" % b], T.cu[:, c0:c0 + 4], T.iu[:, c0:c0 + 3]
+        lists = [("cb", 12), ("co", 16)] if b else [("ca", 8)]
 
-        def m(k, ins):
-            ins.then_inc(S[k + str(b)], 1)
+        def counts():
+            return [sc.activation(T.sg[:, 64 * c:64 * c + 63], T.eb[:, lo + 1:hi], F.Sign, bias=T.thb[:, c:c + 1], scale=-1.0,
+                                  accum_out=T.acc[:, c:c + 1]) for c in range(c0, c0 + 3)]
+        return {
+            "lf": (lists + [("pl", 1)], lambda: pick(q, T.lnf[:, lo:hi], T.tab[:, 0:64].indirect(cu))),
+            "en": (lists + [("pe", 1)], lambda: pick(q, T.eng[:, lo:hi], T.tab[:, 64:128].indirect(cu))),
+            "eb": (["lf"], lambda: v.tensor_tensor_scan(T.eb[:, lo + 1:hi + 1], T.sb[:, lo:hi], T.lnf[:, lo:hi], 0.0, A.max, A.add)),
+            "ac": (["eb", ("th", 1)], counts),
+            "ei": (["eb", ("eb0", 1)], lambda: v.tensor_copy(T.ei[:, lo:hi], T.eb[:, lo:hi])),
+            "bs": (["eb", "en"], lambda: v.tensor_tensor(bs[:, 1:65], T.eng[:, lo:hi], T.eb[:, lo + 1:hi + 1], A.subtract)),
+            "ph": (["ei"], lambda: v.tensor_scalar(T.ph[:, lo:hi], T.ei[:, lo:hi], 15, None, A.bitwise_and)),
+            "jp": (["bs"], lambda: v.tensor_tensor(T.jp[:, lo:hi], bs[:, 1:65], bs[:, 0:64], A.subtract)),
+            "mk": (["ph"], lambda: v.tensor_scalar(T.mk[:, lo:hi], T.ph[:, lo:hi], T.cf[:, 0:1], None, A.is_le)),
+            "iu": ([("ac%d" % b, 3)], lambda: v.tensor_scalar(iu, T.acc[:, c0:c0 + 3], 0.5, 31.5, A.mult, A.add)),
+            "gm": (["jp", "mk"], lambda: v.tensor_tensor(T.gm[:, lo:hi], T.jp[:, lo:hi], T.mk[:, lo:hi], A.mult)),
+            "gg": (["gm"], lambda: v.tensor_tensor_scan(T.gg[:, lo:hi], T.zz[:, :], T.gm[:, lo:hi], 0.0, A.add, A.add)),
+            "hh": (["gm"], lambda: v.tensor_tensor_scan(T.hh[:, lo:hi], T.jp[:, lo:hi], T.gm[:, lo:hi], 0.0, A.add, A.subtract)),
+            "ta": (["iu", "gg"], lambda: v.tensor_tensor(t1[:, 0:48], T.gg[:, lo:hi].indirect(iu), T.cc[:, 48 * b:48 * b + 48], A.add)),
+            "tb": (["ta", "hh"], lambda: v.tensor_tensor(T.t2[:, 48 * b:48 * b + 48], T.hh[:, lo:hi].indirect(iu), t1[:, 1:49], A.add)),
+        }[k]
 
-        def wm(*ks):
-            for k in ks:
-                v.wait_ge(S[k + str(b)], 3 if k == "ac" else 1)
+    def step(q, k):
+        if k == "wq":
+            return [("ldq", 16)], lambda: v.quantize_mx(T.wc[:, :], T.wp[:, :], T.qs[:, :])
+        if k == "tr":
+            return [("ell", 128)], lambda: v.transpose(T.tout[:, :], T.tin[:, :])
+        if k == "eu":
+            return [("tr", 1)], lambda: v.tensor_copy(T.eu[:, :], T.tout[:, 0:8])
+        if k == "sc":
+            return [("eu", 1), ("mz", 1)], lambda: v.tensor_copy(T.msk[:, :].indirect(T.eu[:, :]), T.neg[:, :])
+        if not k[1].isdigit():
+            waits, call = pass_step(q, k[:2], int(k[2]))
+            return [w if isinstance(w, tuple) else (w + k[2], 1) for w in waits], call
+        s = int(k[1])
+        if k[0] == "o":
+            t = int(k[2])
+            return [("tb%d" % s, 1)], lambda: v.tensor_scalar(T["of%d" % t][:, KP * s:KP * s + KP], T.t2[:, 48 * s:48 * s + KP], 4.0,
+                                                            T.cf[:, 2 + t:3 + t], A.mult, A.add)
+        if k[0] == "g":
+            t = int(k[2])
+            return ([("ldx", 64), ("vz", 1), ("o%d%d" % (s // 4, t), 1)],
+                    lambda: pick(q, T.h[:, 640 * s + t:640 * s + 640:4], T.xs[:, 0:4 * XW].indirect(T["of%d" % t][:, 10 * s:10 * s + 10])))
+        if k[0] == "q":
+            cc, pp = (T.rc, T.rp) if s == OWN else (T.qc, T.qp)
+            return [("hg%d" % s, 4)], lambda: v.quantize_mx(cc[:, CAP * s:CAP * s + CAP], pp[:, CAP * s:CAP * s + CAP], T.h[:, 640 * s:640 * s + 640])
+        if k[0] == "z":
+            a, b = CAP * UNITS[s][0], CAP * sum(UNITS[s])
+            return ([("pm%d" % s, 1), ("sc", 1)],
+                    lambda: v.tensor_tensor_scan(T.z[:, a + 1:b + 1], T.msk[:, a:b], T.ps[:, 512 * s:512 * s + b - a], NEG, A.add, A.max))
+        r0 = min(rank_at[c] for c in SLOT[s])
+        end = max(sum(u) for u in UNITS if u[0] <= max(SLOT[s]) < sum(u))
+        return ([("z%d" % u, 1) for u in range(len(UNITS)) if UNITS[u][0] < end],
+                lambda: pick(q, T.ys[:, 16 * r0:16 * r0 + 32], T.z[:, 0:CAP * end + 1].indirect(T.eu[:, r0:r0 + 2])))
 
-        wm("eb")
-        m("ei", v.tensor_copy(T.ei[:, lo:hi], T.eb[:, lo:hi]))
-        wm("en")
-        m("bs", v.tensor_tensor(bs[:, 1:65], T.eng[:, lo:hi], T.eb[:, lo + 1:hi + 1], A.subtract))
-        wm("ei")
-        m("ph", v.tensor_scalar(T.ph[:, lo:hi], T.ei[:, lo:hi], 15, None, A.bitwise_and))
-        wm("bs")
-        m("jp", v.tensor_tensor(T.jp[:, lo:hi], bs[:, 1:65], bs[:, 0:64], A.subtract))
-        wm("ph")
-        m("mk", v.tensor_scalar(T.mk[:, lo:hi], T.ph[:, lo:hi], T.cf[:, 0:1], None, A.is_le))
-        wm("ac")
-        m("iu", v.tensor_scalar(T.iu[:, c0:c0 + 3], T.acc[:, c0:c0 + 3], 0.5, 31.5, A.mult, A.add))
-        wm("jp", "mk")
-        m("gm", v.tensor_tensor(T.gm[:, lo:hi], T.jp[:, lo:hi], T.mk[:, lo:hi], A.mult))
-        between()
-        wm("gm")
-        m("gg", v.tensor_tensor_scan(T.gg[:, lo:hi], T.zz[:, :], T.gm[:, lo:hi], 0.0, A.add, A.add))
-        m("hh", v.tensor_tensor_scan(T.hh[:, lo:hi], T.jp[:, lo:hi], T.gm[:, lo:hi], 0.0, A.add, A.subtract))
-        wm("iu", "gg")
-        m("ta", v.tensor_tensor(t1[:, 0:48], T.gg[:, lo:hi].indirect(T.iu[:, c0:c0 + 3]), T.cc[:, 48 * b:48 * b + 48], A.add))
-        wm("ta", "hh")
-        m("tb", v.tensor_tensor(T.t2[:, 48 * b:48 * b + 48], T.hh[:, lo:hi].indirect(T.iu[:, c0:c0 + 3]), t1[:, 1:49], A.add))
-        wm("tb")
-        for t in range(4):
-            v.tensor_scalar(T["of%d" % t][:, KP * b:KP * b + KP], T.t2[:, 48 * b:48 * b + KP], 4.0, T.cf[:, 2 + t:3 + t],
-                            A.mult, A.add).then_inc(S["of%d%d" % (b, t)], 1)
-
-    seen = {"s": [], "v": []}
-
-    def gather(key, s, t):
-        q = sc if key == "s" else v
-        if not seen[key]:
-            q.wait_ge(S.ldx, 64)
-            q.wait_ge(S.vz, 1)
-        sem = "of%d%d" % (s // 4, t)
-        if sem not in seen[key]:
-            q.wait_ge(S[sem], 1)
-            seen[key].append(sem)
-        out, win = T.h[:, 640 * s + t:640 * s + 640:4], T.xs[:, 0:4 * XW].indirect(T["of%d" % t][:, 10 * s:10 * s + 10])
-        ins = sc.activation(out, win, F.Copy) if key == "s" else v.tensor_copy(out, win)
-        ins.then_inc(S["hg%d" % s], 1)
-
-    def quant(s):
-        v.wait_ge(S["hg%d" % s], 4)
-        cc, pp = (T.rc, T.rp) if s == OWN else (T.qc, T.qp)
-        v.quantize_mx(cc[:, CAP * s:CAP * s + CAP], pp[:, CAP * s:CAP * s + CAP], T.h[:, 640 * s:640 * s + 640]).then_inc(S["qz%d" % s], 1)
-
-    for s in range(8):
-        for t in SCALAR[s]:
-            gather("s", s, t)
-
-    v.wait_ge(S.pb, 1)
-    v.wait_ge(S.ca, 8)
-    v.tensor_copy(T.lnf[:, 0:64], T.tab[:, 0:64].indirect(T.cu[:, 0:4])).then_inc(S.lf0, 1)
-    ends(0)
-    lists(0, lambda: ends(1))
-    gather("v", 0, 2)
-    gather("v", 0, 3)
-    quant(0)
-    lists(1, lambda: quant(1))
-    for s in (2, 4):
-        gather("v", s, 3)
-        gather("v", s + 1, 3)
-        quant(s)
-        gather("v", s + 1, 2)
-        quant(s + 1)
-    gather("v", PAR, 2)
-    gather("v", PAR, 3)
-    quant(PAR)
-    v.wait_ge(S.ldq, 16)
-    v.quantize_mx(T.wc[:, :], T.wp[:, :], T.qs[:, :]).then_inc(S.wq, 1)
+    for q, order in ((v, VECTOR), (sc, SCALAR)):
+        seen = []
+        for k in order.split():
+            waits, call = step(q, k)
+            for w in waits:
+                if w not in seen:
+                    seen.append(w)
+                    q.wait_ge(S[w[0]], w[1])
+            done = call()
+            for ins in (done if isinstance(done, list) else [done]):
+                ins.then_inc(S["hg" + k[1] if k[0] == "g" and k[1].isdigit() else k], 1)
 
     sy.wait_ge(S.eb0, 1)
     sy.wait_ge(S.eb1, 1)
     sy.dma_start(T.es[:, :], T.eb[0:1, 1:W + 1]).then_inc(S.est, 16)
     sy.dma_start(T.el[me, W:W + CD, :], T.eb[0:1, CD * OWN + 1:CD * OWN + CD + 1]).then_inc(S.est, 16)
 
+    def el(s):
+        return T.el[me, W - CD * s:2 * W - CD * s, :]
     g.wait_ge(S.est, 32)
-    g.remote_dma_fused([RemoteDMATransfer(dst_ids=[dst_id(s) for s in range(7)], dma_engine_mask=msk(far_e[0:1]), remote_sem=S.er,
-                                          srcs=[T.es[:, :]], dsts=[T.el[me, W - CD * s:2 * W - CD * s, :] for s in range(7)])],
-                       local_sem=S.ls)
+    g.remote_dma_fused([RemoteDMATransfer(dst_ids=[dst_id(s) for s in range(PAR)], dma_engine_mask=msk(far_e[0:1]), remote_sem=S.er,
+                                          srcs=[T.es[:, :]], dsts=[el(s) for s in range(PAR)]),
+                        tr(PAR, near_e[4:8], "er", T.es[:, :], el(PAR))], local_sem=S.ls)
     sent[0] += 1
 
     def codes(s, es):
@@ -263,52 +240,36 @@ def rank_program(g, core, T, topo):
     def plane(s, es):
         return tr(s, es, "ar%d" % s, T.qp[:, CAP * s:CAP * s + CAP], T.rp[:, CAP * s:CAP * s + CAP])
 
-    for s in range(6):
-        g.wait_ge(S["qz%d" % s], 1)
+    for s in range(PAR):
+        g.wait_ge(S["q%d" % s], 1)
         g.remote_dma_fused([codes(s, far_e)], local_sem=S.ls)
-        if s % 2:
+        if s >= 4:
+            g.remote_dma_fused([plane(s, far_e)], local_sem=S.ls)
+        elif s % 2:
             g.remote_dma_fused([plane(s - 1, far_e[0:4]), plane(s, far_e[4:8])], local_sem=S.ls)
-    g.wait_ge(S["qz%d" % PAR], 1)
+    g.wait_ge(S["q%d" % PAR], 1)
     g.remote_dma_fused([codes(PAR, near_e)], local_sem=S.ls)
     g.remote_dma_fused([plane(PAR, near_e)], local_sem=S.ls)
 
     sy.wait_ge(S.est, 32)
-    sy.wait_ge(S.er, 7)
+    sy.wait_ge(S.er, PAR + 4)
     sy.wait_ge(S.rw, 1)
     for a in range(4):
         for c in (0, CD):
             sy.dma_start(T.tin[32 * a:32 * a + 8, c:c + CD], T.el[:, W:W + CD, :]).then_inc(S.ell, 16)
-    v.wait_ge(S.ell, 128)
-    op(v.transpose(T.tout[:, :], T.tin[:, :]))
-    sync_v()
-    op(v.tensor_copy(T.eu[:, :], T.tout[:, 0:8]))
-    v.wait_ge(S.mz, 1)
-    sync_v()
-    op(v.tensor_copy(T.msk[:, :].indirect(T.eu[:, :]), T.neg[:, :]))
-    sync_v()
 
-    units = [(0, 2), (2, 2), (4, 2), (OWN, 1), (PAR, 1)]
     pe.wait_ge(S.wq, 1)
-    for u, (s0, k) in enumerate(units):
+    for u, (s0, k) in enumerate(UNITS):
         for s in range(s0, s0 + k):
             if s == OWN:
-                pe.wait_ge(S["qz%d" % s], 1)
+                pe.wait_ge(S["q%d" % s], 1)
             else:
-                pe.wait_ge(S["ar%d" % s], 16 if s == PAR else 12)
+                pe.wait_ge(S["ar%d" % s], 16 if s >= 4 else 12)
         a, b = CAP * s0, CAP * (s0 + k)
         pe.matmul_mx(T.ps[:, 512 * u:512 * u + b - a], T.wc[:, :], T.wp[:, :], T.rc[:, a:b], T.rp[:, a:b], True, True).then_inc(S["pm%d" % u], 1)
-    for u, (s0, k) in enumerate(units):
-        a, b = CAP * s0, CAP * (s0 + k)
-        v.wait_ge(S["pm%d" % u], 1)
-        op(v.tensor_tensor_scan(T.z[:, a + 1:b + 1], T.msk[:, a:b], T.ps[:, 512 * u:512 * u + b - a], NEG, A.add, A.max))
-        if u == 0:
-            quant(OWN)
-        if s0 == OWN:
-            continue
-        r0 = min(rank_at[s0], rank_at[s0 + 1])
-        sync_v()
-        v.tensor_copy(T.ys[:, 16 * r0:16 * r0 + 32], T.z[:, 0:a + 2 * CAP + 1].indirect(T.eu[:, r0:r0 + 2])).then_inc(S["yg%d" % u], 1)
-        sy.wait_ge(S["yg%d" % u], 1)
+    for c in range(4):
+        r0 = min(rank_at[s] for s in SLOT[c])
+        sy.wait_ge(S["y%d" % c], 1)
         sy.dma_start(T.y[:, 16 * r0:16 * r0 + 32], T.ys[:, 16 * r0:16 * r0 + 32]).then_inc(S.yd, 16)
     sy.wait_ge(S.yd, 64)
     g.wait_ge(S.ls, sent[0])

@@ -1,47 +1,61 @@
 from concourse.bass import DstId, RemoteDMATransfer
 from concourse.mybir import dt, AluOpType, ActivationFunctionType
 
-N, CD, CAP, XC = 8, 16, 160, 1024
+N, ND, CD, CAP, XC = 8, 64, 16, 160, 1024
 XW = XC + CAP
 NEG = -5.0e29
 W = N * CD
 KP = 4 * CAP // 16
-PAR, OWN = 6, 7
-SLOT = [(0, 1), (2, 4), (3, 5), (PAR, OWN)]
-UNITS = [(0, 2), (2, 2), (OWN, 1), (4, 1), (5, 1), (PAR, 1)]
+OWN, PAR, HLP = 4, 5, 7
+SLOT = [(0, HLP), (1, 3), (2, 6), (PAR, OWN)]
+FAR = [0, 1, 2, 3, 6]
+PASS = [(4, 3), (3, 2)]
+UNITS = [(0, 2), (2, 2), (PAR, 1), (OWN, 1), (6, 1)]
+XQ = {"xa": (0, 512), "xb": (512, 768), "xc": (768, 1024)}
 
-VECTOR = ("lf0 eb0 ei0 bs0 ph0 jp0 mk0 iu0 eb1 gm0 ei1 bs1 gg0 hh0 ph1 ta0 jp1 tb0 mk1 iu1 o00 o01 o02 o03 gm1 "
-          "g02 gg1 hh1 g03 ta1 q0 tb1 g13 o10 o11 o12 o13 q1 g23 g33 q2 g32 g43 q3 g42 g53 q4 g63 q5 g62 wq q6 "
-          "tr g73 eu sc q7 z0 z1 z2 z3 z4 z5 y3")
-SCALAR = ("en0 ac0 lf1 en1 ac1 g00 g01 g10 g11 g12 g20 g21 g22 g30 g31 g40 g41 g50 g51 g52 g60 g61 "
-          "g70 g71 g72 y0 y1 y2")
+VECTOR = ("xa xb lf0 wq eb0 ei0 bs0 ph0 jp0 mk0 iu0 eb1 gm0 ei1 bs1 gg0 hh0 ph1 ta0 jp1 tb0 mk1 iu1 o00 o01 o02 o03 gm1 "
+          "xc g02 gg1 hh1 g03 ta1 q0 tb1 g13 o10 o11 o12 o13 q1 g23 g33 q2 g32 g53 q3 g63 tr q5 g62 eu q6 "
+          "sc z0 q4 z1 z2 z3 z4")
+SCALAR = ("en0 ac0 lf1 en1 ac1 g00 g01 g10 g11 g12 g20 g21 g22 g30 g31 g50 g51 g52 g60 g61 "
+          "g40 g41 g42 g43 y0 y1 y3 y2")
+SENDS = "c0 p0 c1 c2 p12 c3 c5 p35 c6 p6"
 
 SCRATCH = {k: ("sbuf", [128, w], t) for t, ks in {
     "int32": {"cd8": 8, "sl": 128, "ip": 1, "ci": 1, "ei": W, "ph": W},
-    "float32": {"row": 192, "tab": 128, "cf": 8, "th": 8, "thb": 8, "sb": W, "zz": 64, "cc": 96, "acc": 8, "sg": 512,
+    "float32": {"row": 192, "tab": 128, "cf": 8, "th": 8, "thb": 8, "sb": W, "zz": 64, "cc": 96, "acc": 8, "sg": 512, "pad": CD,
                 "lnf": W, "eng": W, "eb": W + 4, "bs0": 68, "bs1": 68, "jp": W, "mk": W, "gm": W, "gg": W, "hh": W,
-                "t10": 52, "t11": 52, "t2": 96, "tin": 32, "tout": 32, "z": 8 * CAP + 8, "ys": 128},
-    "uint16": {"cdu": 8, "cu": 8, "iu": 8, "of0": 2 * KP, "of1": 2 * KP, "of2": 2 * KP, "of3": 2 * KP, "eu": 8},
-    "bfloat16": {"xs": 4 * XW, "h": 32 * CAP, "qs": 512, "msk": 8 * CAP + 8, "neg": 128},
-    "float8_e4m3fn_x4": {"qc": 8 * CAP, "wc": 128, "rc": 8 * CAP},
-    "uint8": {"qp": 8 * CAP, "wp": 128, "rp": 8 * CAP}}.items() for k, w in ks.items()}
+                "t10": 52, "t11": 52, "t2": 96, "tin": 32, "tout": 32, "z": 8 * CAP + 8, "ys": 128,
+                "hf": 8, "he": 4, "zd": ND, "yh": CD, "yp": CD},
+    "uint16": {"cdu": 8, "cu": 8, "iu": 8, "of0": 2 * KP, "of1": 2 * KP, "of2": 2 * KP, "of3": 2 * KP, "eu": 8,
+               "tu": 128, "hs": 8, "hu": 4, "hl": 2},
+    "bfloat16": {"xs": 4 * XW, "h": 28 * CAP, "qs": 512, "msk": 8 * CAP + 8, "neg": 128},
+    "float8_e4m3fn_x4": {"qc": 7 * CAP, "wc": 128, "rc": 7 * CAP, "xq": XC},
+    "uint8": {"qp": 7 * CAP, "wp": 128, "rp": 7 * CAP, "xp": XC}}.items() for k, w in ks.items()}
 SCRATCH["es"] = ("dram", [128, 1], "float32")
 SCRATCH["el"] = ("dram", [8, 256, 1], "float32")
+SCRATCH["ts"] = ("dram", [128, 1], "uint16")
+SCRATCH["td"] = ("dram", [128, 1], "uint16")
 SCRATCH["ps"] = ("psum", [128, len(UNITS) * 512], "float32")
-SEMAPHORES = (["ldc", "ldt", "ldx", "ldq", "gi", "pl", "pe", "vt", "vl", "xgo", "vz", "ca", "cb", "co", "cv", "est", "er", "ell", "yd", "ls",
-               "vv", "th", "mz", "rw"]
-              + ["hg%d" % s for s in range(8)] + ["ar%d" % s for s in range(7)] + ["pm%d" % u for u in range(len(UNITS))]
+SEMAPHORES = (["ldc", "ldt", "lxa", "lxb", "lxc", "ldq", "gi", "pl", "pe", "vt", "vl", "xgo", "vz", "ca", "cb", "co", "cv", "est", "er",
+               "ell", "yd", "ls", "vv", "th", "mz", "rw", "tu", "tst", "pad", "hw", "hxa", "hxb", "hxc", "ht", "hl", "hld", "hy", "hv"]
+              + ["hg%d" % s for s in range(7)] + ["ar%d" % s for s in FAR + [PAR]] + ["pm%d" % u for u in range(len(UNITS))]
               + [k for k in (VECTOR + " " + SCALAR).split() if k[0] != "g" or k[1] in "gm"])
 
 
 def rank_program(g, core, T, topo):
-    me = T.rank_of(core)
-    if me is None:
-        return
     A, F = AluOpType, ActivationFunctionType
     v, sc, sy, pe = g.vector, g.scalar, g.sync, g.tensor
     S = T.sem
     cores = list(T.cores)
+
+    def helper(r):
+        return [c for c in topo.cores_of(cores[r])
+                if c not in cores and topo.die(c) == topo.die(cores[r]) and all(topo.may_write(c, d) for d in cores)][0]
+
+    helped = [r for r in range(N) if helper(r) == core]
+    me = helped[0] if helped else T.rank_of(core)
+    if me is None:
+        return
 
     def dist(a, b):
         ca, cb = topo.chip(a), topo.chip(b)
@@ -60,8 +74,9 @@ def rank_program(g, core, T, topo):
     rank_at = [None] * N
     for r in range(N):
         rank_at[slot(me, r)] = r
-    far_e = topo.engines(core, cores[rank_at[0]])
-    near_e = [e for e in topo.engines(core, cores[rank_at[PAR]]) if e not in far_e]
+    hlp = rank_at[HLP]
+    far_e = topo.engines(core, cores[hlp])
+    near_e = [e for e in topo.engines(cores[me], cores[rank_at[PAR]]) if e not in far_e]
 
     def msk(es):
         m = 0
@@ -69,46 +84,18 @@ def rank_program(g, core, T, topo):
             m |= 1 << e
         return int(m)
 
-    def dst_id(s):
-        rid, pid, _ = topo.addr(cores[rank_at[s]])
+    def dst_id(c):
+        rid, pid, _ = topo.addr(c)
         return DstId(rid=rid, pnc=pid)
 
     sent = [0]
 
-    def tr(s, es, sem, src, dst):
+    def tr(c, es, sem, src, dst):
         sent[0] += len(es)
-        return RemoteDMATransfer(dst_ids=[dst_id(s)], dma_engine_mask=msk(es), remote_sem=S[sem], src=src, dst=dst)
+        return RemoteDMATransfer(dst_ids=[dst_id(c)], dma_engine_mask=msk(es), remote_sem=S[sem], src=src, dst=dst)
 
-    for k in range(8):
-        (sy if k % 2 == 0 else sc).dma_start(T.cd8[16 * k:16 * k + 16, :], T.cd[:, :]).then_inc(S.ldc, 16)
-    sy.dma_start(T.sl[0:1, 0:64], T.st[:, :]).then_inc(S.ldt, 16)
-    sc.dma_start(T.sl[0:1, 64:128], T.ln[:, :]).then_inc(S.ldt, 16)
-    sy.dma_start(T.xs[:, 0:1024], T.x[:, 0:1024]).then_inc(S.ldx, 16)
-    sc.dma_start(T.xs[:, 1024:2048], T.x[:, 1024:2048]).then_inc(S.ldx, 16)
-    sy.wait_ge(S.cv, 1)
-    sy.dma_start(T.cu[:, OWN:OWN + 1], T.cdu[:, me:me + 1]).then_inc(S.co, 16)
-    sy.wait_ge(S.xgo, 1)
-    sy.dma_start(T.xs[:, 2048:3072], T.x[:, 2048:3072]).then_inc(S.ldx, 16)
-    sc.wait_ge(S.xgo, 1)
-    sc.dma_start(T.xs[:, 3072:4096], T.x[:, 3072:4096]).then_inc(S.ldx, 16)
-    sc.dma_start(T.qs[:, :], T.qw[:, :]).then_inc(S.ldq, 16)
-
-    g.iota(T.ip[:, 0:1], [[0, 1]], 0, 1).then_inc(S.gi, 1)
-    for out, pat, base in ((T.th[:, :], [[16 * KP, 2], [256, 4]], 0), (T.sb[:, :], [[CAP, 8], [0, CD]], 0),
-                           (T.cc[:, :], [[16 * KP, 2], [16, 48]], -16)):
-        g.iota(out, pat, base, 0, allow_small_or_imprecise_dtypes=True).then_inc(S.gi, 1)
-    g.wait_ge(S.cv, 1)
-
-    def cdt(s, es, sem):
-        r = rank_at[s]
-        return tr(s, es, sem, T.cdu[:, r:r + 1], T.cu[:, s:s + 1])
-    g.remote_dma_fused([cdt(s, far_e[2 * s:2 * s + 2], "ca") for s in range(4)], local_sem=S.ls)
-    g.remote_dma_fused([cdt(4, far_e[0:4], "cb"), cdt(5, far_e[4:8], "cb"), cdt(PAR, near_e[0:4], "cb")], local_sem=S.ls)
-    g.sem_inc(S.xgo, 1)
-    g.wait_ge(S.vl, 4)
-    g.partition_broadcast(T.tab[:, 0:64], T.row[0:1, 64:128], 128).then_inc(S.pl, 1)
-    g.wait_ge(S.vt, 1)
-    g.partition_broadcast(T.tab[:, 64:128], T.row[0:1, 128:192], 128).then_inc(S.pe, 1)
+    def send(*transfers):
+        g.remote_dma_fused(list(transfers), local_sem=S.ls)
 
     n = {"vv": 0}
 
@@ -119,27 +106,115 @@ def rank_program(g, core, T, topo):
     def sync_v():
         v.wait_ge(S.vv, n["vv"])
 
+    if helped:
+        for q in (sy, sc):
+            q.wait_ge(S.ht, 1)
+        for k in range(8):
+            sy.dma_start(T.hs[16 * k:16 * k + 16, 0:4], T.td[0:ND, :]).then_inc(S.hld, 16)
+            sc.dma_start(T.hs[16 * k:16 * k + 16, 4:8], T.td[ND:2 * ND, :]).then_inc(S.hld, 16)
+        op(v.memset(T.msk[:, :], 0.0))
+        op(v.memset(T.neg[:, :], NEG))
+        op(v.memset(T.z[:, 0:1], NEG))
+        v.wait_ge(S.hld, 256)
+        op(v.tensor_copy(T.hf[:, :], T.hs[:, :]))
+        sync_v()
+        op(v.tensor_copy(T.msk[:, :].indirect(T.hs[:, 0:4]), T.neg[:, 0:ND]))
+        op(v.tensor_tensor(T.he[:, :], T.hf[:, 0:4], T.hf[:, 4:8], A.add))
+        sync_v()
+        op(v.tensor_copy(T.hu[:, :], T.he[:, :]))
+        pe.wait_ge(S.hw, 16)
+        for k, piece in enumerate(XQ):
+            a, b = XQ[piece]
+            out = T.ps[:, 512 * k:512 * k + b - a]
+            pe.wait_ge(S["h" + piece], 16)
+            pe.matmul_mx(out, T.wc[:, :], T.wp[:, :], T.xq[:, a:b], T.xp[:, a:b], True, True).then_inc(S["pm%d" % k], 1)
+            sync_v()
+            v.wait_ge(S["pm%d" % k], 1)
+            op(v.tensor_tensor_scan(T.z[:, a + 1:b + 1], T.msk[:, a:b], out, T.z[:, a:a + 1], A.add, A.max))
+        sync_v()
+        op(v.tensor_copy(T.zd[:, :], T.z[:, 0:XC + 1].indirect(T.hu[:, :])))
+        sync_v()
+        v.wait_ge(S.hl, 4)
+        v.tensor_copy(T.yh[:, :], T.zd[:, :].indirect(T.hl[:, 0:1])).then_inc(S.hv, 1)
+        g.wait_ge(S.hv, 1)
+        send(tr(cores[hlp], far_e[0:4], "hy", T.yh[:, :], T.yp[:, :]))
+        g.wait_ge(S.ls, sent[0])
+        return
+
+    def load_x(q, k, sem):
+        q.dma_start(T.xs[:, 1024 * k:1024 * k + 1024], T.x[:, 1024 * k:1024 * k + 1024]).then_inc(S[sem], 16)
+    for k in range(4):
+        (sy if k % 2 == 0 else sc).dma_start(T.cd8[16 * k:16 * k + 16, :], T.cd[:, :]).then_inc(S.ldc, 16)
+    sy.dma_start(T.sl[0:1, 0:64], T.st[:, :]).then_inc(S.ldt, 16)
+    sc.dma_start(T.sl[0:1, 64:128], T.ln[:, :]).then_inc(S.ldt, 16)
+    load_x(sy, 0, "lxa")
+    load_x(sc, 1, "lxa")
+    sy.dma_start(T.qs[:, :], T.qw[:, :]).then_inc(S.ldq, 16)
+    load_x(sc, 2, "lxb")
+    sy.wait_ge(S.cv, 2)
+    sy.dma_start(T.cu[:, OWN:OWN + 1], T.cdu[:, me:me + 1]).then_inc(S.co, 16)
+    sy.wait_ge(S.tu, 1)
+    sy.dma_start(T.ts[:, :], T.tu[0:1, :]).then_inc(S.tst, 16)
+    sc.wait_ge(S.xgo, 1)
+    load_x(sc, 3, "lxc")
+
+    g.iota(T.ip[:, 0:1], [[0, 1]], 0, 1).then_inc(S.gi, 1)
+    for out, pat, base in ((T.th[:, :], [[16 * KP, 2], [256, 4]], 0), (T.sb[:, :], [[CAP, 8], [0, CD]], 0),
+                           (T.cc[:, :], [[16 * KP, 2], [16, 48]], -16)):
+        g.iota(out, pat, base, 0, allow_small_or_imprecise_dtypes=True).then_inc(S.gi, 1)
+    g.iota(T.pad[:, :], [[1, CD]], HLP * CAP + 1, 0, allow_small_or_imprecise_dtypes=True).then_inc(S.pad, 1)
+    g.wait_ge(S.cv, 2)
+
+    def cdt(s, es, sem):
+        r = rank_at[s]
+        return tr(cores[r], es, sem, T.cdu[:, r:r + 1], T.cu[:, s:s + 1])
+    send(*[cdt(s, far_e[2 * s:2 * s + 2], "ca") for s in range(4)])
+    send(cdt(6, far_e[0:4], "cb"), cdt(PAR, near_e[0:4], "cb"), tr(helper(hlp), far_e[4:8], "hl", T.cdu[:, hlp:hlp + 1], T.hl[:, 0:1]))
+    g.sem_inc(S.xgo, 1)
+    g.wait_ge(S.vl, 4)
+    g.partition_broadcast(T.tab[:, 0:64], T.row[0:1, 64:128], 128).then_inc(S.pl, 1)
+    g.wait_ge(S.vt, 1)
+    g.partition_broadcast(T.tab[:, 64:128], T.row[0:1, 128:192], 128).then_inc(S.pe, 1)
+
+    def x_codes(piece):
+        a, b = XQ[piece]
+        g.wait_ge(S[piece], 1)
+        send(tr(helper(me), near_e, "h" + piece, T.xq[:, a:b].bitcast(dt.uint8), T.xq[:, a:b].bitcast(dt.uint8)))
+        send(tr(helper(me), near_e, "h" + piece, T.xp[:, a:b], T.xp[:, a:b]))
+    g.wait_ge(S.tst, 16)
+    send(tr(helper(me), far_e[0:1], "ht", T.ts[:, :], T.td[:, :]))
+    a, b = XQ["xa"]
+    g.wait_ge(S.xa, 1)
+    send(tr(helper(me), near_e, "hxa", T.xq[:, a:b].bitcast(dt.uint8), T.xq[:, a:b].bitcast(dt.uint8)))
+    g.wait_ge(S.wq, 1)
+    send(tr(helper(hlp), far_e, "hw", T.wc[:, :].bitcast(dt.uint8), T.wc[:, :].bitcast(dt.uint8)),
+         tr(helper(me), near_e, "hxa", T.xp[:, a:b], T.xp[:, a:b]))
+    send(tr(helper(hlp), far_e, "hw", T.wp[:, :], T.wp[:, :]))
+    x_codes("xb")
+
     v.memset(T.tin[:, :], 0.0).then_inc(S.rw, 1)
     op(v.memset(T.zz[:, :], 0.0))
     op(v.memset(T.neg[:, :], NEG))
-    for b, c in (("z", 0), ("eb", 0), ("bs0", 0), ("bs1", 0), ("t10", 48), ("t11", 48)):
-        op(v.memset(T[b][:, c:c + 1], 0.0))
-    v.wait_ge(S.ldc, 128)
-    v.tensor_copy(T.cdu[:, :], T.cd8[:, :]).then_inc(S.cv, 1)
+    for b, c, d in (("z", 0, 1), ("eb", 0, 1), ("eb", 113, W + 1), ("bs0", 0, 1), ("bs1", 0, 1), ("t10", 48, 49), ("t11", 32, 33)):
+        op(v.memset(T[b][:, c:d], 0.0))
+    op(v.memset(T.msk[:, :], 0.0))
+    v.wait_ge(S.ldc, 64)
+    for a in (0, 64):
+        v.tensor_copy(T.cdu[a:a + 64, :], T.cd8[0:64, :]).then_inc(S.cv, 1)
     v.wait_ge(S.gi, 4)
     op(v.tensor_scalar(T.ci[:, 0:1], T.ip[:, 0:1], 15, None, A.bitwise_and))
     v.wait_ge(S.ldt, 32)
+    v.tensor_copy(T.tu[0:1, :], T.sl[0:1, :]).then_inc(S.tu, 1)
     for k in range(4):
         v.tensor_copy(T.row[0:1, 64 + 16 * k:80 + 16 * k], T.sl[0:1, 64 + k:128:4]).then_inc(S.vl, 1)
+    sync_v()
+    op(v.tensor_copy(T.cf[:, 0:1], T.ci[:, 0:1]))
     for k in range(4):
         op(v.tensor_copy(T.row[0:1, 16 * k:16 * k + 16], T.sl[0:1, k:64:4]))
     v.memset(T.xs[:, 4 * XC:4 * XW], 0.0).then_inc(S.vz, 1)
     sync_v()
     v.wait_ge(S.vl, 4)
     v.tensor_tensor(T.row[0:1, 128:192], T.row[0:1, 0:64], T.row[0:1, 64:128], A.add).then_inc(S.vt, 1)
-    op(v.tensor_copy(T.cf[:, 0:1], T.ci[:, 0:1]))
-    op(v.memset(T.msk[:, :], 0.0))
-    sync_v()
     op(v.tensor_scalar(T.cf[:, 1:2], T.cf[:, 0:1], 16.0, -0.5, A.mult, A.add))
     for t in range(4):
         op(v.tensor_scalar(T.cf[:, 2 + t:3 + t], T.cf[:, 0:1], 4.0, float(t), A.mult, A.add))
@@ -151,34 +226,42 @@ def rank_program(g, core, T, topo):
         return v.tensor_copy(out, win) if q is v else sc.activation(out, win, F.Copy)
 
     def pass_step(q, k, b):
-        lo, hi, c0 = 64 * b, 64 * b + 64, 4 * b
-        bs, t1, cu, iu = T["bs%d" % b], T["t1%d" % b], T.cu[:, c0:c0 + 4], T.iu[:, c0:c0 + 3]
-        lists = [("cb", 12), ("co", 16)] if b else [("ca", 8)]
+        slots, cols = PASS[b]
+        nd, nk = CD * slots, 16 * cols
+        lo, hi, c0, k0 = 64 * b, 64 * b + nd, 4 * b, 48 * b
+        bs, t1, cu, iu = T["bs%d" % b], T["t1%d" % b], T.cu[:, c0:c0 + slots], T.iu[:, c0:c0 + cols]
+        lists = [("cb", 8), ("co", 16)] if b else [("ca", 8)]
 
         def counts():
-            return [sc.activation(T.sg[:, 64 * c:64 * c + 63], T.eb[:, lo + 1:hi], F.Sign, bias=T.thb[:, c:c + 1], scale=-1.0,
-                                  accum_out=T.acc[:, c:c + 1]) for c in range(c0, c0 + 3)]
+            return [sc.activation(T.sg[:, 64 * c:64 * c + nd - 1], T.eb[:, lo + 1:hi], F.Sign, bias=T.thb[:, c:c + 1], scale=-1.0,
+                                  accum_out=T.acc[:, c:c + 1]) for c in range(c0, c0 + cols)]
         return {
             "lf": (lists + [("pl", 1)], lambda: pick(q, T.lnf[:, lo:hi], T.tab[:, 0:64].indirect(cu))),
             "en": (lists + [("pe", 1)], lambda: pick(q, T.eng[:, lo:hi], T.tab[:, 64:128].indirect(cu))),
             "eb": (["lf"], lambda: v.tensor_tensor_scan(T.eb[:, lo + 1:hi + 1], T.sb[:, lo:hi], T.lnf[:, lo:hi], 0.0, A.max, A.add)),
             "ac": (["eb", ("th", 1)], counts),
             "ei": (["eb", ("eb0", 1)], lambda: v.tensor_copy(T.ei[:, lo:hi], T.eb[:, lo:hi])),
-            "bs": (["eb", "en"], lambda: v.tensor_tensor(bs[:, 1:65], T.eng[:, lo:hi], T.eb[:, lo + 1:hi + 1], A.subtract)),
+            "bs": (["eb", "en"], lambda: v.tensor_tensor(bs[:, 1:nd + 1], T.eng[:, lo:hi], T.eb[:, lo + 1:hi + 1], A.subtract)),
             "ph": (["ei"], lambda: v.tensor_scalar(T.ph[:, lo:hi], T.ei[:, lo:hi], 15, None, A.bitwise_and)),
-            "jp": (["bs"], lambda: v.tensor_tensor(T.jp[:, lo:hi], bs[:, 1:65], bs[:, 0:64], A.subtract)),
+            "jp": (["bs"], lambda: v.tensor_tensor(T.jp[:, lo:hi], bs[:, 1:nd + 1], bs[:, 0:nd], A.subtract)),
             "mk": (["ph"], lambda: v.tensor_scalar(T.mk[:, lo:hi], T.ph[:, lo:hi], T.cf[:, 0:1], None, A.is_le)),
-            "iu": ([("ac%d" % b, 3)], lambda: v.tensor_scalar(iu, T.acc[:, c0:c0 + 3], 0.5, 31.5, A.mult, A.add)),
+            "iu": ([("ac%d" % b, cols)], lambda: v.tensor_scalar(iu, T.acc[:, c0:c0 + cols], 0.5, (nd - 1) / 2, A.mult, A.add)),
             "gm": (["jp", "mk"], lambda: v.tensor_tensor(T.gm[:, lo:hi], T.jp[:, lo:hi], T.mk[:, lo:hi], A.mult)),
-            "gg": (["gm"], lambda: v.tensor_tensor_scan(T.gg[:, lo:hi], T.zz[:, :], T.gm[:, lo:hi], 0.0, A.add, A.add)),
+            "gg": (["gm"], lambda: v.tensor_tensor_scan(T.gg[:, lo:hi], T.zz[:, 0:nd], T.gm[:, lo:hi], 0.0, A.add, A.add)),
             "hh": (["gm"], lambda: v.tensor_tensor_scan(T.hh[:, lo:hi], T.jp[:, lo:hi], T.gm[:, lo:hi], 0.0, A.add, A.subtract)),
-            "ta": (["iu", "gg"], lambda: v.tensor_tensor(t1[:, 0:48], T.gg[:, lo:hi].indirect(iu), T.cc[:, 48 * b:48 * b + 48], A.add)),
-            "tb": (["ta", "hh"], lambda: v.tensor_tensor(T.t2[:, 48 * b:48 * b + 48], T.hh[:, lo:hi].indirect(iu), t1[:, 1:49], A.add)),
+            "ta": (["iu", "gg"], lambda: v.tensor_tensor(t1[:, 0:nk], T.gg[:, lo:hi].indirect(iu), T.cc[:, k0:k0 + nk], A.add)),
+            "tb": (["ta", "hh"], lambda: v.tensor_tensor(T.t2[:, k0:k0 + nk], T.hh[:, lo:hi].indirect(iu), t1[:, 1:nk + 1], A.add)),
         }[k]
+
+    def y_place(c):
+        return min(rank_at[s] for s in SLOT[c]), len([s for s in SLOT[c] if s != HLP])
 
     def step(q, k):
         if k == "wq":
             return [("ldq", 16)], lambda: v.quantize_mx(T.wc[:, :], T.wp[:, :], T.qs[:, :])
+        if k in XQ:
+            a, b = XQ[k]
+            return [("l" + k, 16 if a else 32)], lambda: v.quantize_mx(T.xq[:, a:b], T.xp[:, a:b], T.xs[:, 4 * a:4 * b])
         if k == "tr":
             return [("ell", 128)], lambda: v.transpose(T.tout[:, :], T.tin[:, :])
         if k == "eu":
@@ -190,12 +273,12 @@ def rank_program(g, core, T, topo):
             return [w if isinstance(w, tuple) else (w + k[2], 1) for w in waits], call
         s = int(k[1])
         if k[0] == "o":
-            t = int(k[2])
-            return [("tb%d" % s, 1)], lambda: v.tensor_scalar(T["of%d" % t][:, KP * s:KP * s + KP], T.t2[:, 48 * s:48 * s + KP], 4.0,
+            t, nk = int(k[2]), 10 * PASS[s][0]
+            return [("tb%d" % s, 1)], lambda: v.tensor_scalar(T["of%d" % t][:, KP * s:KP * s + nk], T.t2[:, 48 * s:48 * s + nk], 4.0,
                                                             T.cf[:, 2 + t:3 + t], A.mult, A.add)
         if k[0] == "g":
             t = int(k[2])
-            return ([("ldx", 64), ("vz", 1), ("o%d%d" % (s // 4, t), 1)],
+            return ([("lxa", 32), ("lxb", 16), ("lxc", 16), ("vz", 1), ("o%d%d" % (s // 4, t), 1)],
                     lambda: pick(q, T.h[:, 640 * s + t:640 * s + 640:4], T.xs[:, 0:4 * XW].indirect(T["of%d" % t][:, 10 * s:10 * s + 10])))
         if k[0] == "q":
             cc, pp = (T.rc, T.rp) if s == OWN else (T.qc, T.qp)
@@ -204,10 +287,11 @@ def rank_program(g, core, T, topo):
             a, b = CAP * UNITS[s][0], CAP * sum(UNITS[s])
             return ([("pm%d" % s, 1), ("sc", 1)],
                     lambda: v.tensor_tensor_scan(T.z[:, a + 1:b + 1], T.msk[:, a:b], T.ps[:, 512 * s:512 * s + b - a], NEG, A.add, A.max))
-        r0 = min(rank_at[c] for c in SLOT[s])
-        end = max(sum(u) for u in UNITS if u[0] <= max(SLOT[s]) < sum(u))
+        r0, k2 = y_place(s)
+        last = max(c for c in SLOT[s] if c != HLP)
+        end = max(sum(u) for u in UNITS if u[0] <= last < sum(u))
         return ([("z%d" % u, 1) for u in range(len(UNITS)) if UNITS[u][0] < end],
-                lambda: pick(q, T.ys[:, 16 * r0:16 * r0 + 32], T.z[:, 0:CAP * end + 1].indirect(T.eu[:, r0:r0 + 2])))
+                lambda: pick(q, T.ys[:, CD * r0:CD * (r0 + k2)], T.z[:, 0:CAP * end + 1].indirect(T.eu[:, r0:r0 + k2])))
 
     for q, order in ((v, VECTOR), (sc, SCALAR)):
         seen = []
@@ -225,34 +309,37 @@ def rank_program(g, core, T, topo):
     sy.wait_ge(S.eb1, 1)
     sy.dma_start(T.es[:, :], T.eb[0:1, 1:W + 1]).then_inc(S.est, 16)
     sy.dma_start(T.el[me, W:W + CD, :], T.eb[0:1, CD * OWN + 1:CD * OWN + CD + 1]).then_inc(S.est, 16)
+    sy.wait_ge(S.pad, 1)
+    sy.dma_start(T.el[y_place(0)[0] + 1, W:W + CD, :], T.pad[0:1, :]).then_inc(S.est, 16)
 
     def el(s):
-        return T.el[me, W - CD * s:2 * W - CD * s, :]
-    g.wait_ge(S.est, 32)
-    g.remote_dma_fused([RemoteDMATransfer(dst_ids=[dst_id(s) for s in range(PAR)], dma_engine_mask=msk(far_e[0:1]), remote_sem=S.er,
-                                          srcs=[T.es[:, :]], dsts=[el(s) for s in range(PAR)]),
-                        tr(PAR, near_e[4:8], "er", T.es[:, :], el(PAR))], local_sem=S.ls)
+        return T.el[me - place(me) if s in SLOT[0] else me, W - CD * s:2 * W - CD * s, :]
+    g.wait_ge(S.est, 48)
+    send(RemoteDMATransfer(dst_ids=[dst_id(cores[rank_at[s]]) for s in FAR + [PAR]], dma_engine_mask=msk(far_e[0:1]), remote_sem=S.er,
+                           srcs=[T.es[:, :]], dsts=[el(s) for s in FAR + [PAR]]))
     sent[0] += 1
 
-    def codes(s, es):
-        return tr(s, es, "ar%d" % s, T.qc[:, CAP * s:CAP * s + CAP].bitcast(dt.uint8), T.rc[:, CAP * s:CAP * s + CAP].bitcast(dt.uint8))
+    def piece(kind, s, es):
+        a, b = CAP * s, CAP * s + CAP
+        if kind == "p":
+            return tr(cores[rank_at[s]], es, "ar%d" % s, T.qp[:, a:b], T.rp[:, a:b])
+        return tr(cores[rank_at[s]], es, "ar%d" % s, T.qc[:, a:b].bitcast(dt.uint8), T.rc[:, a:b].bitcast(dt.uint8))
 
-    def plane(s, es):
-        return tr(s, es, "ar%d" % s, T.qp[:, CAP * s:CAP * s + CAP], T.rp[:, CAP * s:CAP * s + CAP])
+    x_codes("xc")
+    arrivals = {}
+    for k in SENDS.split():
+        slots = [int(c) for c in k[1:]]
+        far = [s for s in slots if s != PAR]
+        share = len(far_e) // max(1, len(far))
+        engines = {s: far_e[share * far.index(s):share * far.index(s) + share] if s in far else near_e for s in slots}
+        for s in slots:
+            if s not in arrivals:
+                g.wait_ge(S["q%d" % s], 1)
+            arrivals[s] = arrivals.get(s, 0) + len(engines[s])
+        send(*[piece(k[0], s, engines[s]) for s in slots])
 
-    for s in range(PAR):
-        g.wait_ge(S["q%d" % s], 1)
-        g.remote_dma_fused([codes(s, far_e)], local_sem=S.ls)
-        if s >= 4:
-            g.remote_dma_fused([plane(s, far_e)], local_sem=S.ls)
-        elif s % 2:
-            g.remote_dma_fused([plane(s - 1, far_e[0:4]), plane(s, far_e[4:8])], local_sem=S.ls)
-    g.wait_ge(S["q%d" % PAR], 1)
-    g.remote_dma_fused([codes(PAR, near_e)], local_sem=S.ls)
-    g.remote_dma_fused([plane(PAR, near_e)], local_sem=S.ls)
-
-    sy.wait_ge(S.est, 32)
-    sy.wait_ge(S.er, PAR + 4)
+    sy.wait_ge(S.est, 48)
+    sy.wait_ge(S.er, len(FAR) + 1)
     sy.wait_ge(S.rw, 1)
     for a in range(4):
         for c in (0, CD):
@@ -264,12 +351,16 @@ def rank_program(g, core, T, topo):
             if s == OWN:
                 pe.wait_ge(S["q%d" % s], 1)
             else:
-                pe.wait_ge(S["ar%d" % s], 16 if s >= 4 else 12)
+                pe.wait_ge(S["ar%d" % s], arrivals[s])
         a, b = CAP * s0, CAP * (s0 + k)
         pe.matmul_mx(T.ps[:, 512 * u:512 * u + b - a], T.wc[:, :], T.wp[:, :], T.rc[:, a:b], T.rp[:, a:b], True, True).then_inc(S["pm%d" % u], 1)
-    for c in range(4):
-        r0 = min(rank_at[s] for s in SLOT[c])
+
+    for c in (0, 1, 3, 2):
+        r0, k2 = y_place(c)
+        r = r0 if k2 == 2 else rank_at[SLOT[c][0]]
         sy.wait_ge(S["y%d" % c], 1)
-        sy.dma_start(T.y[:, 16 * r0:16 * r0 + 32], T.ys[:, 16 * r0:16 * r0 + 32]).then_inc(S.yd, 16)
-    sy.wait_ge(S.yd, 64)
+        sy.dma_start(T.y[:, CD * r:CD * (r + k2)], T.ys[:, CD * r0:CD * (r0 + k2)]).then_inc(S.yd, 16)
+    sc.wait_ge(S.hy, 4)
+    sc.dma_start(T.y[:, CD * hlp:CD * hlp + CD], T.yp[:, :]).then_inc(S.yd, 16)
+    sy.wait_ge(S.yd, 80)
     g.wait_ge(S.ls, sent[0])

from concourse.bass import DstId, RemoteDMATransfer
from concourse.mybir import dt, AluOpType, ActivationFunctionType

N, ND, CD, CAP, XC = 8, 64, 16, 160, 1024
XW = XC + CAP
NEG = -5.0e29
W = N * CD
KP = 4 * CAP // 16
OWN, PAR, HLP = 4, 5, 7
SLOT = [(0, HLP), (1, 3), (2, 6), (PAR, OWN)]
FAR = [0, 1, 2, 3, 6]
PASS = [(4, 3), (3, 2)]
UNITS = [(0, 2), (2, 2), (PAR, 1), (OWN, 1), (6, 1)]
XQ = {"xa": (0, 512), "xb": (512, 768), "xc": (768, 1024)}

VECTOR = ("xa xb lf0 wq eb0 ei0 bs0 ph0 jp0 mk0 iu0 eb1 gm0 ei1 bs1 gg0 hh0 ph1 ta0 jp1 tb0 mk1 iu1 o00 o01 o02 o03 gm1 "
          "xc g02 gg1 hh1 g03 ta1 q0 tb1 g13 o10 o11 o12 o13 q1 g23 g33 q2 g32 g53 q3 g63 tr q5 g62 eu q6 "
          "sc z0 q4 z1 z2 z3 z4")
SCALAR = ("en0 ac0 lf1 en1 ac1 g00 g01 g10 g11 g12 g20 g21 g22 g30 g31 g50 g51 g52 g60 g61 "
          "g40 g41 g42 g43 y0 y1 y3 y2")
SENDS = "c0 p0 c1 c2 p12 c3 c5 p35 c6 p6"

SCRATCH = {k: ("sbuf", [128, w], t) for t, ks in {
    "int32": {"cd8": 8, "sl": 128, "ip": 1, "ci": 1, "ei": W, "ph": W},
    "float32": {"row": 192, "tab": 128, "cf": 8, "th": 8, "thb": 8, "sb": W, "zz": 64, "cc": 96, "acc": 8, "sg": 512, "pad": CD,
                "lnf": W, "eng": W, "eb": W + 4, "bs0": 68, "bs1": 68, "jp": W, "mk": W, "gm": W, "gg": W, "hh": W,
                "t10": 52, "t11": 52, "t2": 96, "tin": 32, "tout": 32, "z": 8 * CAP + 8, "ys": 128,
                "hf": 8, "he": 4, "zd": ND, "yh": CD, "yp": CD},
    "uint16": {"cdu": 8, "cu": 8, "iu": 8, "of0": 2 * KP, "of1": 2 * KP, "of2": 2 * KP, "of3": 2 * KP, "eu": 8,
               "tu": 128, "hs": 8, "hu": 4, "hl": 2},
    "bfloat16": {"xs": 4 * XW, "h": 28 * CAP, "qs": 512, "msk": 8 * CAP + 8, "neg": 128},
    "float8_e4m3fn_x4": {"qc": 7 * CAP, "wc": 128, "rc": 7 * CAP, "xq": XC},
    "uint8": {"qp": 7 * CAP, "wp": 128, "rp": 7 * CAP, "xp": XC}}.items() for k, w in ks.items()}
SCRATCH["es"] = ("dram", [128, 1], "float32")
SCRATCH["el"] = ("dram", [8, 256, 1], "float32")
SCRATCH["ts"] = ("dram", [128, 1], "uint16")
SCRATCH["td"] = ("dram", [128, 1], "uint16")
SCRATCH["ps"] = ("psum", [128, len(UNITS) * 512], "float32")
SEMAPHORES = (["ldc", "ldt", "lxa", "lxb", "lxc", "ldq", "gi", "pl", "pe", "vt", "vl", "xgo", "vz", "ca", "cb", "co", "cv", "est", "er",
               "ell", "yd", "ls", "vv", "th", "mz", "rw", "tu", "tst", "pad", "hw", "hxa", "hxb", "hxc", "ht", "hl", "hld", "hy", "hv"]
              + ["hg%d" % s for s in range(7)] + ["ar%d" % s for s in FAR + [PAR]] + ["pm%d" % u for u in range(len(UNITS))]
              + [k for k in (VECTOR + " " + SCALAR).split() if k[0] != "g" or k[1] in "gm"])


def rank_program(g, core, T, topo):
    A, F = AluOpType, ActivationFunctionType
    v, sc, sy, pe = g.vector, g.scalar, g.sync, g.tensor
    S = T.sem
    cores = list(T.cores)

    def helper(r):
        return [c for c in topo.cores_of(cores[r])
                if c not in cores and topo.die(c) == topo.die(cores[r]) and all(topo.may_write(c, d) for d in cores)][0]

    helped = [r for r in range(N) if helper(r) == core]
    me = helped[0] if helped else T.rank_of(core)
    if me is None:
        return

    def dist(a, b):
        ca, cb = topo.chip(a), topo.chip(b)
        if ca == cb:
            return 3
        if topo.mates(ca, cb):
            return 2
        return 1 if topo.same_plane(ca, cb) else 0

    def place(r):
        return [k for k in range(N) if topo.chip(cores[k]) == topo.chip(cores[r])].index(r)

    def slot(a, b):
        return SLOT[dist(cores[a], cores[b])][int(place(a) == place(b))]

    rank_at = [None] * N
    for r in range(N):
        rank_at[slot(me, r)] = r
    hlp = rank_at[HLP]
    far_e = topo.engines(core, cores[hlp])
    near_e = [e for e in topo.engines(cores[me], cores[rank_at[PAR]]) if e not in far_e]

    def msk(es):
        m = 0
        for e in es:
            m |= 1 << e
        return int(m)

    def dst_id(c):
        rid, pid, _ = topo.addr(c)
        return DstId(rid=rid, pnc=pid)

    sent = [0]

    def tr(c, es, sem, src, dst):
        sent[0] += len(es)
        return RemoteDMATransfer(dst_ids=[dst_id(c)], dma_engine_mask=msk(es), remote_sem=S[sem], src=src, dst=dst)

    def send(*transfers):
        g.remote_dma_fused(list(transfers), local_sem=S.ls)

    n = {"vv": 0}

    def op(ins):
        ins.then_inc(S.vv, 1)
        n["vv"] += 1

    def sync_v():
        v.wait_ge(S.vv, n["vv"])

    if helped:
        for q in (sy, sc):
            q.wait_ge(S.ht, 1)
        for k in range(8):
            sy.dma_start(T.hs[16 * k:16 * k + 16, 0:4], T.td[0:ND, :]).then_inc(S.hld, 16)
            sc.dma_start(T.hs[16 * k:16 * k + 16, 4:8], T.td[ND:2 * ND, :]).then_inc(S.hld, 16)
        op(v.memset(T.msk[:, :], 0.0))
        op(v.memset(T.neg[:, :], NEG))
        op(v.memset(T.z[:, 0:1], NEG))
        v.wait_ge(S.hld, 256)
        op(v.tensor_copy(T.hf[:, :], T.hs[:, :]))
        sync_v()
        op(v.tensor_copy(T.msk[:, :].indirect(T.hs[:, 0:4]), T.neg[:, 0:ND]))
        op(v.tensor_tensor(T.he[:, :], T.hf[:, 0:4], T.hf[:, 4:8], A.add))
        sync_v()
        op(v.tensor_copy(T.hu[:, :], T.he[:, :]))
        pe.wait_ge(S.hw, 16)
        for k, piece in enumerate(XQ):
            a, b = XQ[piece]
            out = T.ps[:, 512 * k:512 * k + b - a]
            pe.wait_ge(S["h" + piece], 16)
            pe.matmul_mx(out, T.wc[:, :], T.wp[:, :], T.xq[:, a:b], T.xp[:, a:b], True, True).then_inc(S["pm%d" % k], 1)
            sync_v()
            v.wait_ge(S["pm%d" % k], 1)
            op(v.tensor_tensor_scan(T.z[:, a + 1:b + 1], T.msk[:, a:b], out, T.z[:, a:a + 1], A.add, A.max))
        sync_v()
        op(v.tensor_copy(T.zd[:, :], T.z[:, 0:XC + 1].indirect(T.hu[:, :])))
        sync_v()
        v.wait_ge(S.hl, 4)
        v.tensor_copy(T.yh[:, :], T.zd[:, :].indirect(T.hl[:, 0:1])).then_inc(S.hv, 1)
        g.wait_ge(S.hv, 1)
        send(tr(cores[hlp], far_e[0:4], "hy", T.yh[:, :], T.yp[:, :]))
        g.wait_ge(S.ls, sent[0])
        return

    def load_x(q, k, sem):
        q.dma_start(T.xs[:, 1024 * k:1024 * k + 1024], T.x[:, 1024 * k:1024 * k + 1024]).then_inc(S[sem], 16)
    for k in range(4):
        (sy if k % 2 == 0 else sc).dma_start(T.cd8[16 * k:16 * k + 16, :], T.cd[:, :]).then_inc(S.ldc, 16)
    sy.dma_start(T.sl[0:1, 0:64], T.st[:, :]).then_inc(S.ldt, 16)
    sc.dma_start(T.sl[0:1, 64:128], T.ln[:, :]).then_inc(S.ldt, 16)
    load_x(sy, 0, "lxa")
    load_x(sc, 1, "lxa")
    sy.dma_start(T.qs[:, :], T.qw[:, :]).then_inc(S.ldq, 16)
    load_x(sc, 2, "lxb")
    sy.wait_ge(S.cv, 2)
    sy.dma_start(T.cu[:, OWN:OWN + 1], T.cdu[:, me:me + 1]).then_inc(S.co, 16)
    sy.wait_ge(S.tu, 1)
    sy.dma_start(T.ts[:, :], T.tu[0:1, :]).then_inc(S.tst, 16)
    sc.wait_ge(S.xgo, 1)
    load_x(sc, 3, "lxc")

    g.iota(T.ip[:, 0:1], [[0, 1]], 0, 1).then_inc(S.gi, 1)
    for out, pat, base in ((T.th[:, :], [[16 * KP, 2], [256, 4]], 0), (T.sb[:, :], [[CAP, 8], [0, CD]], 0),
                           (T.cc[:, :], [[16 * KP, 2], [16, 48]], -16)):
        g.iota(out, pat, base, 0, allow_small_or_imprecise_dtypes=True).then_inc(S.gi, 1)
    g.iota(T.pad[:, :], [[1, CD]], HLP * CAP + 1, 0, allow_small_or_imprecise_dtypes=True).then_inc(S.pad, 1)
    g.wait_ge(S.cv, 2)

    def cdt(s, es, sem):
        r = rank_at[s]
        return tr(cores[r], es, sem, T.cdu[:, r:r + 1], T.cu[:, s:s + 1])
    send(*[cdt(s, far_e[2 * s:2 * s + 2], "ca") for s in range(4)])
    send(cdt(6, far_e[0:4], "cb"), cdt(PAR, near_e[0:4], "cb"), tr(helper(hlp), far_e[4:8], "hl", T.cdu[:, hlp:hlp + 1], T.hl[:, 0:1]))
    g.sem_inc(S.xgo, 1)
    g.wait_ge(S.vl, 4)
    g.partition_broadcast(T.tab[:, 0:64], T.row[0:1, 64:128], 128).then_inc(S.pl, 1)
    g.wait_ge(S.vt, 1)
    g.partition_broadcast(T.tab[:, 64:128], T.row[0:1, 128:192], 128).then_inc(S.pe, 1)

    def x_codes(piece):
        a, b = XQ[piece]
        g.wait_ge(S[piece], 1)
        send(tr(helper(me), near_e, "h" + piece, T.xq[:, a:b].bitcast(dt.uint8), T.xq[:, a:b].bitcast(dt.uint8)))
        send(tr(helper(me), near_e, "h" + piece, T.xp[:, a:b], T.xp[:, a:b]))
    g.wait_ge(S.tst, 16)
    send(tr(helper(me), far_e[0:1], "ht", T.ts[:, :], T.td[:, :]))
    a, b = XQ["xa"]
    g.wait_ge(S.xa, 1)
    send(tr(helper(me), near_e, "hxa", T.xq[:, a:b].bitcast(dt.uint8), T.xq[:, a:b].bitcast(dt.uint8)))
    g.wait_ge(S.wq, 1)
    send(tr(helper(hlp), far_e, "hw", T.wc[:, :].bitcast(dt.uint8), T.wc[:, :].bitcast(dt.uint8)),
         tr(helper(me), near_e, "hxa", T.xp[:, a:b], T.xp[:, a:b]))
    send(tr(helper(hlp), far_e, "hw", T.wp[:, :], T.wp[:, :]))
    x_codes("xb")

    v.memset(T.tin[:, :], 0.0).then_inc(S.rw, 1)
    op(v.memset(T.zz[:, :], 0.0))
    op(v.memset(T.neg[:, :], NEG))
    for b, c, d in (("z", 0, 1), ("eb", 0, 1), ("eb", 113, W + 1), ("bs0", 0, 1), ("bs1", 0, 1), ("t10", 48, 49), ("t11", 32, 33)):
        op(v.memset(T[b][:, c:d], 0.0))
    op(v.memset(T.msk[:, :], 0.0))
    v.wait_ge(S.ldc, 64)
    for a in (0, 64):
        v.tensor_copy(T.cdu[a:a + 64, :], T.cd8[0:64, :]).then_inc(S.cv, 1)
    v.wait_ge(S.gi, 4)
    op(v.tensor_scalar(T.ci[:, 0:1], T.ip[:, 0:1], 15, None, A.bitwise_and))
    v.wait_ge(S.ldt, 32)
    v.tensor_copy(T.tu[0:1, :], T.sl[0:1, :]).then_inc(S.tu, 1)
    for k in range(4):
        v.tensor_copy(T.row[0:1, 64 + 16 * k:80 + 16 * k], T.sl[0:1, 64 + k:128:4]).then_inc(S.vl, 1)
    sync_v()
    op(v.tensor_copy(T.cf[:, 0:1], T.ci[:, 0:1]))
    for k in range(4):
        op(v.tensor_copy(T.row[0:1, 16 * k:16 * k + 16], T.sl[0:1, k:64:4]))
    v.memset(T.xs[:, 4 * XC:4 * XW], 0.0).then_inc(S.vz, 1)
    sync_v()
    v.wait_ge(S.vl, 4)
    v.tensor_tensor(T.row[0:1, 128:192], T.row[0:1, 0:64], T.row[0:1, 64:128], A.add).then_inc(S.vt, 1)
    op(v.tensor_scalar(T.cf[:, 1:2], T.cf[:, 0:1], 16.0, -0.5, A.mult, A.add))
    for t in range(4):
        op(v.tensor_scalar(T.cf[:, 2 + t:3 + t], T.cf[:, 0:1], 4.0, float(t), A.mult, A.add))
    v.tensor_copy(T.msk[:, 0:8 * CAP:CAP], T.neg[:, 0:8]).then_inc(S.mz, 1)
    sync_v()
    v.tensor_scalar(T.thb[:, :], T.th[:, :], T.cf[:, 1:2], None, A.add).then_inc(S.th, 1)

    def pick(q, out, win):
        return v.tensor_copy(out, win) if q is v else sc.activation(out, win, F.Copy)

    def pass_step(q, k, b):
        slots, cols = PASS[b]
        nd, nk = CD * slots, 16 * cols
        lo, hi, c0, k0 = 64 * b, 64 * b + nd, 4 * b, 48 * b
        bs, t1, cu, iu = T["bs%d" % b], T["t1%d" % b], T.cu[:, c0:c0 + slots], T.iu[:, c0:c0 + cols]
        lists = [("cb", 8), ("co", 16)] if b else [("ca", 8)]

        def counts():
            return [sc.activation(T.sg[:, 64 * c:64 * c + nd - 1], T.eb[:, lo + 1:hi], F.Sign, bias=T.thb[:, c:c + 1], scale=-1.0,
                                  accum_out=T.acc[:, c:c + 1]) for c in range(c0, c0 + cols)]
        return {
            "lf": (lists + [("pl", 1)], lambda: pick(q, T.lnf[:, lo:hi], T.tab[:, 0:64].indirect(cu))),
            "en": (lists + [("pe", 1)], lambda: pick(q, T.eng[:, lo:hi], T.tab[:, 64:128].indirect(cu))),
            "eb": (["lf"], lambda: v.tensor_tensor_scan(T.eb[:, lo + 1:hi + 1], T.sb[:, lo:hi], T.lnf[:, lo:hi], 0.0, A.max, A.add)),
            "ac": (["eb", ("th", 1)], counts),
            "ei": (["eb", ("eb0", 1)], lambda: v.tensor_copy(T.ei[:, lo:hi], T.eb[:, lo:hi])),
            "bs": (["eb", "en"], lambda: v.tensor_tensor(bs[:, 1:nd + 1], T.eng[:, lo:hi], T.eb[:, lo + 1:hi + 1], A.subtract)),
            "ph": (["ei"], lambda: v.tensor_scalar(T.ph[:, lo:hi], T.ei[:, lo:hi], 15, None, A.bitwise_and)),
            "jp": (["bs"], lambda: v.tensor_tensor(T.jp[:, lo:hi], bs[:, 1:nd + 1], bs[:, 0:nd], A.subtract)),
            "mk": (["ph"], lambda: v.tensor_scalar(T.mk[:, lo:hi], T.ph[:, lo:hi], T.cf[:, 0:1], None, A.is_le)),
            "iu": ([("ac%d" % b, cols)], lambda: v.tensor_scalar(iu, T.acc[:, c0:c0 + cols], 0.5, (nd - 1) / 2, A.mult, A.add)),
            "gm": (["jp", "mk"], lambda: v.tensor_tensor(T.gm[:, lo:hi], T.jp[:, lo:hi], T.mk[:, lo:hi], A.mult)),
            "gg": (["gm"], lambda: v.tensor_tensor_scan(T.gg[:, lo:hi], T.zz[:, 0:nd], T.gm[:, lo:hi], 0.0, A.add, A.add)),
            "hh": (["gm"], lambda: v.tensor_tensor_scan(T.hh[:, lo:hi], T.jp[:, lo:hi], T.gm[:, lo:hi], 0.0, A.add, A.subtract)),
            "ta": (["iu", "gg"], lambda: v.tensor_tensor(t1[:, 0:nk], T.gg[:, lo:hi].indirect(iu), T.cc[:, k0:k0 + nk], A.add)),
            "tb": (["ta", "hh"], lambda: v.tensor_tensor(T.t2[:, k0:k0 + nk], T.hh[:, lo:hi].indirect(iu), t1[:, 1:nk + 1], A.add)),
        }[k]

    def y_place(c):
        return min(rank_at[s] for s in SLOT[c]), len([s for s in SLOT[c] if s != HLP])

    def step(q, k):
        if k == "wq":
            return [("ldq", 16)], lambda: v.quantize_mx(T.wc[:, :], T.wp[:, :], T.qs[:, :])
        if k in XQ:
            a, b = XQ[k]
            return [("l" + k, 16 if a else 32)], lambda: v.quantize_mx(T.xq[:, a:b], T.xp[:, a:b], T.xs[:, 4 * a:4 * b])
        if k == "tr":
            return [("ell", 128)], lambda: v.transpose(T.tout[:, :], T.tin[:, :])
        if k == "eu":
            return [("tr", 1)], lambda: v.tensor_copy(T.eu[:, :], T.tout[:, 0:8])
        if k == "sc":
            return [("eu", 1), ("mz", 1)], lambda: v.tensor_copy(T.msk[:, :].indirect(T.eu[:, :]), T.neg[:, :])
        if not k[1].isdigit():
            waits, call = pass_step(q, k[:2], int(k[2]))
            return [w if isinstance(w, tuple) else (w + k[2], 1) for w in waits], call
        s = int(k[1])
        if k[0] == "o":
            t, nk = int(k[2]), 10 * PASS[s][0]
            return [("tb%d" % s, 1)], lambda: v.tensor_scalar(T["of%d" % t][:, KP * s:KP * s + nk], T.t2[:, 48 * s:48 * s + nk], 4.0,
                                                            T.cf[:, 2 + t:3 + t], A.mult, A.add)
        if k[0] == "g":
            t = int(k[2])
            return ([("lxa", 32), ("lxb", 16), ("lxc", 16), ("vz", 1), ("o%d%d" % (s // 4, t), 1)],
                    lambda: pick(q, T.h[:, 640 * s + t:640 * s + 640:4], T.xs[:, 0:4 * XW].indirect(T["of%d" % t][:, 10 * s:10 * s + 10])))
        if k[0] == "q":
            cc, pp = (T.rc, T.rp) if s == OWN else (T.qc, T.qp)
            return [("hg%d" % s, 4)], lambda: v.quantize_mx(cc[:, CAP * s:CAP * s + CAP], pp[:, CAP * s:CAP * s + CAP], T.h[:, 640 * s:640 * s + 640])
        if k[0] == "z":
            a, b = CAP * UNITS[s][0], CAP * sum(UNITS[s])
            return ([("pm%d" % s, 1), ("sc", 1)],
                    lambda: v.tensor_tensor_scan(T.z[:, a + 1:b + 1], T.msk[:, a:b], T.ps[:, 512 * s:512 * s + b - a], NEG, A.add, A.max))
        r0, k2 = y_place(s)
        last = max(c for c in SLOT[s] if c != HLP)
        end = max(sum(u) for u in UNITS if u[0] <= last < sum(u))
        return ([("z%d" % u, 1) for u in range(len(UNITS)) if UNITS[u][0] < end],
                lambda: pick(q, T.ys[:, CD * r0:CD * (r0 + k2)], T.z[:, 0:CAP * end + 1].indirect(T.eu[:, r0:r0 + k2])))

    for q, order in ((v, VECTOR), (sc, SCALAR)):
        seen = []
        for k in order.split():
            waits, call = step(q, k)
            for w in waits:
                if w not in seen:
                    seen.append(w)
                    q.wait_ge(S[w[0]], w[1])
            done = call()
            for ins in (done if isinstance(done, list) else [done]):
                ins.then_inc(S["hg" + k[1] if k[0] == "g" and k[1].isdigit() else k], 1)

    sy.wait_ge(S.eb0, 1)
    sy.wait_ge(S.eb1, 1)
    sy.dma_start(T.es[:, :], T.eb[0:1, 1:W + 1]).then_inc(S.est, 16)
    sy.dma_start(T.el[me, W:W + CD, :], T.eb[0:1, CD * OWN + 1:CD * OWN + CD + 1]).then_inc(S.est, 16)
    sy.wait_ge(S.pad, 1)
    sy.dma_start(T.el[y_place(0)[0] + 1, W:W + CD, :], T.pad[0:1, :]).then_inc(S.est, 16)

    def el(s):
        return T.el[me - place(me) if s in SLOT[0] else me, W - CD * s:2 * W - CD * s, :]
    g.wait_ge(S.est, 48)
    send(RemoteDMATransfer(dst_ids=[dst_id(cores[rank_at[s]]) for s in FAR + [PAR]], dma_engine_mask=msk(far_e[0:1]), remote_sem=S.er,
                           srcs=[T.es[:, :]], dsts=[el(s) for s in FAR + [PAR]]))
    sent[0] += 1

    def piece(kind, s, es):
        a, b = CAP * s, CAP * s + CAP
        if kind == "p":
            return tr(cores[rank_at[s]], es, "ar%d" % s, T.qp[:, a:b], T.rp[:, a:b])
        return tr(cores[rank_at[s]], es, "ar%d" % s, T.qc[:, a:b].bitcast(dt.uint8), T.rc[:, a:b].bitcast(dt.uint8))

    x_codes("xc")
    arrivals = {}
    for k in SENDS.split():
        slots = [int(c) for c in k[1:]]
        far = [s for s in slots if s != PAR]
        share = len(far_e) // max(1, len(far))
        engines = {s: far_e[share * far.index(s):share * far.index(s) + share] if s in far else near_e for s in slots}
        for s in slots:
            if s not in arrivals:
                g.wait_ge(S["q%d" % s], 1)
            arrivals[s] = arrivals.get(s, 0) + len(engines[s])
        send(*[piece(k[0], s, engines[s]) for s in slots])

    sy.wait_ge(S.est, 48)
    sy.wait_ge(S.er, len(FAR) + 1)
    sy.wait_ge(S.rw, 1)
    for a in range(4):
        for c in (0, CD):
            sy.dma_start(T.tin[32 * a:32 * a + 8, c:c + CD], T.el[:, W:W + CD, :]).then_inc(S.ell, 16)

    pe.wait_ge(S.wq, 1)
    for u, (s0, k) in enumerate(UNITS):
        for s in range(s0, s0 + k):
            if s == OWN:
                pe.wait_ge(S["q%d" % s], 1)
            else:
                pe.wait_ge(S["ar%d" % s], arrivals[s])
        a, b = CAP * s0, CAP * (s0 + k)
        pe.matmul_mx(T.ps[:, 512 * u:512 * u + b - a], T.wc[:, :], T.wp[:, :], T.rc[:, a:b], T.rp[:, a:b], True, True).then_inc(S["pm%d" % u], 1)

    for c in (0, 1, 3, 2):
        r0, k2 = y_place(c)
        r = r0 if k2 == 2 else rank_at[SLOT[c][0]]
        sy.wait_ge(S["y%d" % c], 1)
        sy.dma_start(T.y[:, CD * r:CD * (r + k2)], T.ys[:, CD * r0:CD * (r0 + k2)]).then_inc(S.yd, 16)
    sc.wait_ge(S.hy, 4)
    sc.dma_start(T.y[:, CD * hlp:CD * hlp + CD], T.yp[:, :]).then_inc(S.yd, 16)
    sy.wait_ge(S.yd, 80)
    g.wait_ge(S.ls, sent[0])
